import numpy as np
import ml_dtypes


def mxq(x, axis, fmt="e4m3"):
    dtype, down = {"e4m3": (ml_dtypes.float8_e4m3fn, 7), "e5m2": (ml_dtypes.float8_e5m2, 14)}[fmt]
    v = np.moveaxis(np.asarray(x, np.float32).astype(ml_dtypes.bfloat16).astype(np.float64), axis, -1)
    blocks = v.reshape(v.shape[:-1] + (-1, 32))
    amax = np.abs(blocks).max(-1, keepdims=True)
    byte = np.maximum(np.where(amax > 0, np.frexp(amax)[1] - 1 + 127, 0) - down, 1)
    scale = np.exp2(byte - 127.0)
    codes = (blocks / scale).astype(np.float32).astype(dtype).astype(np.float64)
    return np.moveaxis((codes * scale).reshape(v.shape), -1, axis)


WIDE = False


def mx_kscale(k):
    if not WIDE:
        return np.ones(k)
    levels = np.array([10, -10, 5, -5, 0])
    if k % 512:
        return np.exp2(np.random.permutation(np.resize(levels, k // 32))).repeat(32)
    a = np.empty((k // 512, 16))
    for p in range(k // 512):
        a[p, :8] = np.random.permutation(np.resize(levels, 8))
        for g in range(8):
            far = levels[np.abs(levels - a[p, g]) >= 10]
            a[p, g + 8] = far[np.random.randint(len(far))]
    return np.exp2(a.ravel()).repeat(32)


def f64(x):
    return np.asarray(x).astype(np.float64)


def striped(idx):
    return np.tile(idx.reshape(-1, 16).T, (8, 1)).astype(np.uint16)


def unstriped(offs):
    return offs[:16].T.reshape(-1).astype(np.int64)


def pack_weight(w):
    k, n = w.shape
    w = f64(np.asarray(w, np.float32).astype(ml_dtypes.bfloat16)).reshape(k // 32, 32, n)
    amax = np.abs(w).max(1)
    byte = np.clip(np.where(amax > 0, np.frexp(amax)[1] - 1 + 127 - 7, 1), 1, 254)
    scaled = (w * np.exp2(127.0 - byte)[:, None, :]).reshape(k, n).astype(np.float32)
    words = np.ascontiguousarray(scaled.reshape(k // 512, 128, 4, n).transpose(0, 1, 3, 2)).astype(ml_dtypes.float8_e4m3fn).view(np.uint8)
    return words, np.ascontiguousarray(byte.astype(np.uint8).reshape(k // 512, 16, n))


def unpack_weight(words, scales):
    g, p, n, _ = words.shape
    vals = np.ascontiguousarray(words).view(ml_dtypes.float8_e4m3fn).astype(np.float64) * np.repeat(np.exp2(scales.astype(np.float64) - 127.0), 8, axis=1)[..., None]
    return vals.transpose(0, 1, 3, 2).reshape(g * 512, n)


K, T, S, N = 1024, 2048, 1024, 128
P = 2 ** 7


def setup_inputs():
    n = np.random.standard_normal
    s = mx_kscale(K)[:, None]
    packed_xT = pack_weight(n((K, T)) * s)
    return {
        "x_words": packed_xT[0],
        "x_scales": packed_xT[1],
        "gate": np.tile(np.random.uniform(0.2, 1.0, T), (P, 1)).astype(np.float32),
        "w1": (n((K, N)) / np.sqrt(K) / s).astype(np.float32),
        "offs": striped(np.random.permutation(T)[:S]),
    }


def reference(x_words, x_scales, gate, w1, offs):
    xq = unpack_weight(x_words, x_scales)[:, unstriped(offs)]
    y = mxq(f64(w1), 0, "e4m3").T @ xq
    g = f64(gate)[:1][:, unstriped(offs)]
    out = np.zeros((N, T))
    out[:, unstriped(offs)] = y * g
    return out

@@ -1,0 +1,96 @@
+from contextlib import ExitStack
+
+import concourse.mybir as mybir
+
+K, T, S, N = 1024, 2048, 1024, 128
+FLOPS = 2 * K * S * N
+
+F32 = mybir.dt.float32
+BF16 = mybir.dt.bfloat16
+I32 = mybir.dt.int32
+U32 = mybir.dt.uint32
+U16 = mybir.dt.uint16
+U8 = mybir.dt.uint8
+FP8X4 = mybir.dt.float8_e4m3fn_x4
+
+P = 128
+PACK = 4
+PASSES = K // (P * PACK)
+HALF = 512
+LIST_COLS = 16
+
+
+def tile_picked_modgate_linnone_p_kernel(tc, x_words, x_scales, gate, w1, offs, out):
+    nc = tc.nc
+    with ExitStack() as ctx:
+        keep = ctx.enter_context(tc.tile_pool(name="keep", bufs=1))
+        psum = ctx.enter_context(tc.psum_pool(name="psum", bufs=1))
+
+        offsets = keep.tile([P, S // LIST_COLS], U16, name="offsets")
+        nc.sync.dma_start(offsets[:], offs)
+
+        scale_table = keep.tile([P, T], U8, name="scale_table", align_bytes=64)
+        nc.vector.memset(scale_table[:].bitcast(I32), 0)
+        for q in range(4):
+            nc.sync.dma_start(
+                scale_table[32 * q : 32 * q + 4 * PASSES, :].bitcast(I32),
+                x_scales[:, 4 * q : 4 * q + 4, :].bitcast(I32),
+            )
+
+        word_tables = [keep.tile([P, T], I32, name=f"word_table{z}", align_bytes=64) for z in range(PASSES)]
+        w_raw = keep.tile([P, PASSES, PACK, N], F32, name="w_raw")
+        gate_table = keep.tile([P, T], F32, name="gate_table", align_bytes=64)
+
+        def load_words(z):
+            nc.sync.dma_start(word_tables[z][:], x_words[z].rearrange("p t r -> p (t r)").bitcast(I32))
+
+        load_words(0)
+        nc.sync.dma_start(
+            w_raw[:].rearrange("p z j n -> p z (j n)"),
+            w1.rearrange("(z p j) n -> p z (j n)", z=PASSES, j=PACK),
+        )
+        load_words(1)
+        nc.sync.dma_start(gate_table[:], gate)
+
+        window = keep.tile([P, T], F32, name="window", align_bytes=64)
+        nc.vector.memset(window[:], 0.0)
+
+        picked_scales = keep.tile([P, S], U8, name="picked_scales", align_bytes=64)
+        nc.vector.tensor_copy(picked_scales[:], scale_table[:].indirect(offsets[:]))
+
+        picked0 = keep.tile([P, S], U32, name="picked0", align_bytes=64)
+        nc.vector.tensor_copy(picked0[:], word_tables[0][:].bitcast(U32).indirect(offsets[:]))
+
+        w_grouped = keep.tile([P, PASSES, N, PACK], BF16, name="w_grouped", align_bytes=64)
+        nc.scalar.copy(w_grouped[:], w_raw[:].rearrange("p z j n -> p z n j"))
+        w_codes = keep.tile([P, PASSES * N], U32, name="w_codes", align_bytes=64)
+        w_scales = keep.tile([P, PASSES * N], U8, name="w_scales", align_bytes=64)
+        nc.vector.quantize_mx(
+            out=w_codes[:].bitcast(FP8X4),
+            scales=w_scales[:],
+            in_=w_grouped[:].rearrange("p z n j -> p (z n j)"),
+        )
+
+        y = keep.tile([P, S], F32, name="y", align_bytes=64)
+        for h in range(S // HALF):
+            cols = slice(h * HALF, (h + 1) * HALF)
+            list_cols = slice(h * HALF // LIST_COLS, (h + 1) * HALF // LIST_COLS)
+            picked1 = keep.tile([P, HALF], U32, name=f"picked1_{h}", align_bytes=64)
+            nc.vector.tensor_copy(picked1[:], word_tables[1][:].bitcast(U32).indirect(offsets[:, list_cols]))
+            acc = psum.tile([P, HALF], F32, name=f"acc{h}")
+            for z, words in enumerate((picked0[:, cols], picked1[:])):
+                nc.tensor.matmul_mx(
+                    out=acc[:],
+                    lhsT=w_codes[:, z * N : (z + 1) * N].bitcast(FP8X4),
+                    lhsT_scale=w_scales[:, z * N : (z + 1) * N],
+                    rhs=words.bitcast(FP8X4),
+                    rhs_scale=picked_scales[4 * z : P, cols],
+                    start=(z == 0),
+                    stop=(z == PASSES - 1),
+                )
+            nc.scalar.copy(y[:, cols], acc[:])
+
+        picked_gate = keep.tile([P, S], F32, name="picked_gate", align_bytes=64)
+        nc.vector.tensor_copy(picked_gate[:], gate_table[:].indirect(offsets[:]))
+        nc.vector.tensor_tensor(window[:].indirect(offsets[:]), y[:], picked_gate[:], mybir.AluOpType.mult)
+        nc.sync.dma_start(out, window[:])

@@ -31,37 +31,36 @@ def tile_picked_modgate_linnone_p_kernel(tc, x_words, x_scales, gate, w1, offs, 
 
         scale_table = keep.tile([P, T], U8, name="scale_table", align_bytes=64)
         nc.vector.memset(scale_table[:].bitcast(I32), 0)
+
+        word_tables = [
+            keep.tile([P, T], I32, name=f"word_table{z}", tag=f"table{z}", align_bytes=64) for z in range(PASSES)
+        ]
+        for z in range(PASSES):
+            nc.sync.dma_start(word_tables[z][:], x_words[z].rearrange("p t r -> p (t r)").bitcast(I32))
+        w_raw = keep.tile([P, PASSES, PACK, N], F32, name="w_raw")
+        nc.sync.dma_start(
+            w_raw[:].rearrange("p z j n -> p z (j n)"),
+            w1.rearrange("(z p j) n -> p z (j n)", z=PASSES, j=PACK),
+        )
         for q in range(4):
             nc.sync.dma_start(
                 scale_table[32 * q : 32 * q + 4 * PASSES, :].bitcast(I32),
                 x_scales[:, 4 * q : 4 * q + 4, :].bitcast(I32),
             )
 
-        word_tables = [keep.tile([P, T], I32, name=f"word_table{z}", align_bytes=64) for z in range(PASSES)]
-        w_raw = keep.tile([P, PASSES, PACK, N], F32, name="w_raw")
-        gate_table = keep.tile([P, T], F32, name="gate_table", align_bytes=64)
-
-        def load_words(z):
-            nc.sync.dma_start(word_tables[z][:], x_words[z].rearrange("p t r -> p (t r)").bitcast(I32))
-
-        load_words(0)
-        nc.sync.dma_start(
-            w_raw[:].rearrange("p z j n -> p z (j n)"),
-            w1.rearrange("(z p j) n -> p z (j n)", z=PASSES, j=PACK),
-        )
-        load_words(1)
-        nc.sync.dma_start(gate_table[:], gate)
-
         window = keep.tile([P, T], F32, name="window", align_bytes=64)
         nc.vector.memset(window[:], 0.0)
 
-        picked_scales = keep.tile([P, S], U8, name="picked_scales", align_bytes=64)
-        nc.vector.tensor_copy(picked_scales[:], scale_table[:].indirect(offsets[:]))
+        picked_words = []
+        for z in range(PASSES):
+            picked = keep.tile([P, S], U32, name=f"picked_words{z}", align_bytes=64)
+            nc.vector.tensor_copy(picked[:], word_tables[z][:].bitcast(U32).indirect(offsets[:]))
+            picked_words.append(picked)
 
-        picked0 = keep.tile([P, S], U32, name="picked0", align_bytes=64)
-        nc.vector.tensor_copy(picked0[:], word_tables[0][:].bitcast(U32).indirect(offsets[:]))
+        gate_table = keep.tile([P, T], F32, name="gate_table", tag="table0", align_bytes=64)
+        nc.sync.dma_start(gate_table[:], gate)
 
-        w_grouped = keep.tile([P, PASSES, N, PACK], BF16, name="w_grouped", align_bytes=64)
+        w_grouped = keep.tile([P, PASSES, N, PACK], BF16, name="w_grouped", tag="staging", align_bytes=64)
         nc.scalar.copy(w_grouped[:], w_raw[:].rearrange("p z j n -> p z n j"))
         w_codes = keep.tile([P, PASSES * N], U32, name="w_codes", align_bytes=64)
         w_scales = keep.tile([P, PASSES * N], U8, name="w_scales", align_bytes=64)
@@ -75,16 +74,16 @@ def tile_picked_modgate_linnone_p_kernel(tc, x_words, x_scales, gate, w1, offs, 
         for h in range(S // HALF):
             cols = slice(h * HALF, (h + 1) * HALF)
             list_cols = slice(h * HALF // LIST_COLS, (h + 1) * HALF // LIST_COLS)
-            picked1 = keep.tile([P, HALF], U32, name=f"picked1_{h}", align_bytes=64)
-            nc.vector.tensor_copy(picked1[:], word_tables[1][:].bitcast(U32).indirect(offsets[:, list_cols]))
+            picked_scales = keep.tile([P, HALF], U8, name=f"picked_scales{h}", tag=("scales0", "staging")[h], align_bytes=64)
+            nc.vector.tensor_copy(picked_scales[:], scale_table[:].indirect(offsets[:, list_cols]))
             acc = psum.tile([P, HALF], F32, name=f"acc{h}")
-            for z, words in enumerate((picked0[:, cols], picked1[:])):
+            for z in range(PASSES):
                 nc.tensor.matmul_mx(
                     out=acc[:],
                     lhsT=w_codes[:, z * N : (z + 1) * N].bitcast(FP8X4),
                     lhsT_scale=w_scales[:, z * N : (z + 1) * N],
-                    rhs=words.bitcast(FP8X4),
-                    rhs_scale=picked_scales[4 * z : P, cols],
+                    rhs=picked_words[z][:, cols].bitcast(FP8X4),
+                    rhs_scale=picked_scales[4 * z : P, :],
                     start=(z == 0),
                     stop=(z == PASSES - 1),
                 )

@@ -60,7 +60,10 @@ def tile_picked_modgate_linnone_p_kernel(tc, x_words, x_scales, gate, w1, offs, 
         gate_table = keep.tile([P, T], F32, name="gate_table", tag="table0", align_bytes=64)
         nc.sync.dma_start(gate_table[:], gate)
 
-        w_grouped = keep.tile([P, PASSES, N, PACK], BF16, name="w_grouped", tag="staging", align_bytes=64)
+        picked_scales = keep.tile([P, S], U8, name="picked_scales", align_bytes=64)
+        nc.vector.tensor_copy(picked_scales[:], scale_table[:].indirect(offsets[:]))
+
+        w_grouped = keep.tile([P, PASSES, N, PACK], BF16, name="w_grouped", align_bytes=64)
         nc.scalar.copy(w_grouped[:], w_raw[:].rearrange("p z j n -> p z n j"))
         w_codes = keep.tile([P, PASSES * N], U32, name="w_codes", align_bytes=64)
         w_scales = keep.tile([P, PASSES * N], U8, name="w_scales", align_bytes=64)
@@ -70,12 +73,10 @@ def tile_picked_modgate_linnone_p_kernel(tc, x_words, x_scales, gate, w1, offs, 
             in_=w_grouped[:].rearrange("p z n j -> p (z n j)"),
         )
 
-        y = keep.tile([P, S], F32, name="y", align_bytes=64)
+        halves = []
         for h in range(S // HALF):
             cols = slice(h * HALF, (h + 1) * HALF)
-            list_cols = slice(h * HALF // LIST_COLS, (h + 1) * HALF // LIST_COLS)
-            picked_scales = keep.tile([P, HALF], U8, name=f"picked_scales{h}", tag=("scales0", "staging")[h], align_bytes=64)
-            nc.vector.tensor_copy(picked_scales[:], scale_table[:].indirect(offsets[:, list_cols]))
+            entries = offsets[:, h * HALF // LIST_COLS : (h + 1) * HALF // LIST_COLS]
             acc = psum.tile([P, HALF], F32, name=f"acc{h}")
             for z in range(PASSES):
                 nc.tensor.matmul_mx(
@@ -83,13 +84,16 @@ def tile_picked_modgate_linnone_p_kernel(tc, x_words, x_scales, gate, w1, offs, 
                     lhsT=w_codes[:, z * N : (z + 1) * N].bitcast(FP8X4),
                     lhsT_scale=w_scales[:, z * N : (z + 1) * N],
                     rhs=picked_words[z][:, cols].bitcast(FP8X4),
-                    rhs_scale=picked_scales[4 * z : P, :],
+                    rhs_scale=picked_scales[4 * z : P, cols],
                     start=(z == 0),
                     stop=(z == PASSES - 1),
                 )
-            nc.scalar.copy(y[:, cols], acc[:])
+            y = keep.tile([P, HALF], F32, name=f"y{h}", align_bytes=64)
+            nc.scalar.copy(y[:], acc[:])
+            picked_gate = keep.tile([P, HALF], F32, name=f"picked_gate{h}", align_bytes=64)
+            nc.vector.tensor_copy(picked_gate[:], gate_table[:].indirect(entries))
+            halves.append((entries, y, picked_gate))
 
-        picked_gate = keep.tile([P, S], F32, name="picked_gate", align_bytes=64)
-        nc.vector.tensor_copy(picked_gate[:], gate_table[:].indirect(offsets[:]))
-        nc.vector.tensor_tensor(window[:].indirect(offsets[:]), y[:], picked_gate[:], mybir.AluOpType.mult)
+        for entries, y, picked_gate in halves:
+            nc.vector.tensor_tensor(window[:].indirect(entries), y[:], picked_gate[:], mybir.AluOpType.mult)
         nc.sync.dma_start(out, window[:])

@@ -1,6 +1,7 @@
 from contextlib import ExitStack
 
 import concourse.mybir as mybir
+from concourse.masks import make_identity
 
 K, T, S, N = 1024, 2048, 1024, 128
 FLOPS = 2 * K * S * N
@@ -16,7 +17,7 @@ FP8X4 = mybir.dt.float8_e4m3fn_x4
 P = 128
 PACK = 4
 PASSES = K // (P * PACK)
-HALF = 512
+BANK = 512
 LIST_COLS = 16
 
 
@@ -29,14 +30,18 @@ def tile_picked_modgate_linnone_p_kernel(tc, x_words, x_scales, gate, w1, offs, 
         offsets = keep.tile([P, S // LIST_COLS], U16, name="offsets")
         nc.sync.dma_start(offsets[:], offs)
 
+        def entries(lo, hi):
+            return offsets[:, lo // LIST_COLS : hi // LIST_COLS]
+
+        gate_table = keep.tile([P, T], F32, name="gate_table", tag="table1", align_bytes=64)
+        nc.sync.dma_start(gate_table[P - 1 : P, :], gate[0:1, :])
+        nc.vector.memset(gate_table[0 : P - 1, :], 0.0)
+
         scale_table = keep.tile([P, T], U8, name="scale_table", align_bytes=64)
         nc.vector.memset(scale_table[:].bitcast(I32), 0)
 
-        word_tables = [
-            keep.tile([P, T], I32, name=f"word_table{z}", tag=f"table{z}", align_bytes=64) for z in range(PASSES)
-        ]
-        for z in range(PASSES):
-            nc.sync.dma_start(word_tables[z][:], x_words[z].rearrange("p t r -> p (t r)").bitcast(I32))
+        word_table0 = keep.tile([P, T], I32, name="word_table0", align_bytes=64)
+        nc.sync.dma_start(word_table0[:], x_words[0].rearrange("p t r -> p (t r)").bitcast(I32))
         w_raw = keep.tile([P, PASSES, PACK, N], F32, name="w_raw")
         nc.sync.dma_start(
             w_raw[:].rearrange("p z j n -> p z (j n)"),
@@ -48,20 +53,22 @@ def tile_picked_modgate_linnone_p_kernel(tc, x_words, x_scales, gate, w1, offs, 
                 x_scales[:, 4 * q : 4 * q + 4, :].bitcast(I32),
             )
 
+        identity = keep.tile([P, P], F32, name="identity")
+        make_identity(nc, identity[:])
+
+        zero = keep.tile([P, 1], F32, name="zero")
+        nc.gpsimd.memset(zero[:], 0.0)
         window = keep.tile([P, T], F32, name="window", align_bytes=64)
-        nc.vector.memset(window[:], 0.0)
+        nc.scalar.copy(window[:], zero[:].to_broadcast([P, T]))
 
-        picked_words = []
-        for z in range(PASSES):
-            picked = keep.tile([P, S], U32, name=f"picked_words{z}", align_bytes=64)
-            nc.vector.tensor_copy(picked[:], word_tables[z][:].bitcast(U32).indirect(offsets[:]))
-            picked_words.append(picked)
+        gate_row = keep.tile([P, S], F32, name="gate_row", align_bytes=64)
+        nc.vector.tensor_copy(gate_row[:], gate_table[:].indirect(offsets[:]))
 
-        gate_table = keep.tile([P, T], F32, name="gate_table", tag="table0", align_bytes=64)
-        nc.sync.dma_start(gate_table[:], gate)
+        word_table1 = keep.tile([P, T], I32, name="word_table1", tag="table1", align_bytes=64)
+        nc.sync.dma_start(word_table1[:], x_words[1].rearrange("p t r -> p (t r)").bitcast(I32))
 
-        picked_scales = keep.tile([P, S], U8, name="picked_scales", align_bytes=64)
-        nc.vector.tensor_copy(picked_scales[:], scale_table[:].indirect(offsets[:]))
+        picked_words0 = keep.tile([P, S], U32, name="picked_words0", align_bytes=64)
+        nc.vector.tensor_copy(picked_words0[:], word_table0[:].bitcast(U32).indirect(offsets[:]))
 
         w_grouped = keep.tile([P, PASSES, N, PACK], BF16, name="w_grouped", align_bytes=64)
         nc.scalar.copy(w_grouped[:], w_raw[:].rearrange("p z j n -> p z n j"))
@@ -73,27 +80,42 @@ def tile_picked_modgate_linnone_p_kernel(tc, x_words, x_scales, gate, w1, offs, 
             in_=w_grouped[:].rearrange("p z n j -> p (z n j)"),
         )
 
-        halves = []
-        for h in range(S // HALF):
-            cols = slice(h * HALF, (h + 1) * HALF)
-            entries = offsets[:, h * HALF // LIST_COLS : (h + 1) * HALF // LIST_COLS]
-            acc = psum.tile([P, HALF], F32, name=f"acc{h}")
-            for z in range(PASSES):
+        picked_scales = keep.tile([P, S], U8, name="picked_scales", align_bytes=64)
+        nc.vector.tensor_copy(picked_scales[:], scale_table[:].indirect(offsets[:]))
+
+        per_bank = BANK // P
+        picked_gate = keep.tile([P, S], F32, name="picked_gate", align_bytes=64)
+        for h in range(S // BANK):
+            turned = psum.tile([P, per_bank, P], F32, name=f"turned{h}")
+            for c in range(per_bank):
+                lo = h * BANK + c * P
+                nc.tensor.transpose(turned[:, c, :], gate_row[:, lo : lo + P], identity[:])
+            gate_col = keep.tile([P, per_bank], F32, name=f"gate_col{h}")
+            nc.scalar.copy(gate_col[:], turned[:, :, P - 1])
+            spread = psum.tile([P, per_bank, P], F32, name=f"spread{h}")
+            for c in range(per_bank):
+                nc.tensor.transpose(spread[:, c, :], gate_col[:, c : c + 1].to_broadcast([P, P]), identity[:])
+            nc.scalar.copy(picked_gate[:, h * BANK : (h + 1) * BANK], spread[:].rearrange("p c n -> p (c n)"))
+
+        y = keep.tile([P, S], F32, name="y", align_bytes=64)
+        for i, (lo, hi) in enumerate([(0, 256), (256, 768), (768, 1024)]):
+            picked_words1 = keep.tile([P, hi - lo], U32, name=f"picked_words1_{i}", align_bytes=64)
+            nc.vector.tensor_copy(picked_words1[:], word_table1[:].bitcast(U32).indirect(entries(lo, hi)))
+            acc = psum.tile([P, hi - lo], F32, name=f"acc{i}")
+            for z, words in enumerate((picked_words0[:, lo:hi], picked_words1[:])):
                 nc.tensor.matmul_mx(
                     out=acc[:],
                     lhsT=w_codes[:, z * N : (z + 1) * N].bitcast(FP8X4),
                     lhsT_scale=w_scales[:, z * N : (z + 1) * N],
-                    rhs=picked_words[z][:, cols].bitcast(FP8X4),
-                    rhs_scale=picked_scales[4 * z : P, cols],
+                    rhs=words.bitcast(FP8X4),
+                    rhs_scale=picked_scales[4 * z : P, lo:hi],
                     start=(z == 0),
                     stop=(z == PASSES - 1),
                 )
-            y = keep.tile([P, HALF], F32, name=f"y{h}", align_bytes=64)
-            nc.scalar.copy(y[:], acc[:])
-            picked_gate = keep.tile([P, HALF], F32, name=f"picked_gate{h}", align_bytes=64)
-            nc.vector.tensor_copy(picked_gate[:], gate_table[:].indirect(entries))
-            halves.append((entries, y, picked_gate))
+            nc.scalar.copy(y[:, lo:hi], acc[:])
 
-        for entries, y, picked_gate in halves:
-            nc.vector.tensor_tensor(window[:].indirect(entries), y[:], picked_gate[:], mybir.AluOpType.mult)
+        for lo, hi in [(0, 256), (256, S)]:
+            nc.vector.tensor_tensor(
+                window[:].indirect(entries(lo, hi)), y[:, lo:hi], picked_gate[:, lo:hi], mybir.AluOpType.mult
+            )
         nc.sync.dma_start(out, window[:])

@@ -33,12 +33,19 @@ def tile_picked_modgate_linnone_p_kernel(tc, x_words, x_scales, gate, w1, offs, 
         def entries(lo, hi):
             return offsets[:, lo // LIST_COLS : hi // LIST_COLS]
 
-        gate_table = keep.tile([P, T], F32, name="gate_table", tag="table1", align_bytes=64)
+        gate_table = keep.tile([P, T], F32, name="gate_table", align_bytes=64)
         nc.sync.dma_start(gate_table[P - 1 : P, :], gate[0:1, :])
         nc.vector.memset(gate_table[0 : P - 1, :], 0.0)
 
         scale_table = keep.tile([P, T], U8, name="scale_table", align_bytes=64)
-        nc.vector.memset(scale_table[:].bitcast(I32), 0)
+        for z in range(PASSES):
+            nc.sync.dma_start(
+                scale_table[96 + 16 * z : 112 + 16 * z, :].bitcast(I32),
+                x_scales[z].bitcast(I32).rearrange("(q r) c -> r q c", r=4),
+            )
+        nc.vector.memset(scale_table[0:96, :].bitcast(I32), 0)
+        picked_scales = keep.tile([P, S], U8, name="picked_scales", align_bytes=64)
+        nc.vector.memset(picked_scales[:].bitcast(I32), 0)
 
         word_table0 = keep.tile([P, T], I32, name="word_table0", align_bytes=64)
         nc.sync.dma_start(word_table0[:], x_words[0].rearrange("p t r -> p (t r)").bitcast(I32))
@@ -47,11 +54,8 @@ def tile_picked_modgate_linnone_p_kernel(tc, x_words, x_scales, gate, w1, offs, 
             w_raw[:].rearrange("p z j n -> p z (j n)"),
             w1.rearrange("(z p j) n -> p z (j n)", z=PASSES, j=PACK),
         )
-        for q in range(4):
-            nc.sync.dma_start(
-                scale_table[32 * q : 32 * q + 4 * PASSES, :].bitcast(I32),
-                x_scales[:, 4 * q : 4 * q + 4, :].bitcast(I32),
-            )
+        word_table1 = keep.tile([P, T], I32, name="word_table1", align_bytes=64)
+        nc.sync.dma_start(word_table1[:], x_words[1].rearrange("p t r -> p (t r)").bitcast(I32))
 
         identity = keep.tile([P, P], F32, name="identity")
         make_identity(nc, identity[:])
@@ -64,8 +68,13 @@ def tile_picked_modgate_linnone_p_kernel(tc, x_words, x_scales, gate, w1, offs, 
         gate_row = keep.tile([P, S], F32, name="gate_row", align_bytes=64)
         nc.vector.tensor_copy(gate_row[:], gate_table[:].indirect(offsets[:]))
 
-        word_table1 = keep.tile([P, T], I32, name="word_table1", tag="table1", align_bytes=64)
-        nc.sync.dma_start(word_table1[:], x_words[1].rearrange("p t r -> p (t r)").bitcast(I32))
+        picked_rows = keep.tile([P, S], U8, name="picked_rows", align_bytes=64)
+        nc.vector.tensor_copy(picked_rows[:], scale_table[:].indirect(offsets[:]))
+        for q in range(4):
+            nc.sync.dma_start(
+                picked_scales[32 * q : 32 * q + 4 * PASSES, :].bitcast(I32),
+                picked_rows[96 + q : P : 4, :].bitcast(I32),
+            )
 
         picked_words0 = keep.tile([P, S], U32, name="picked_words0", align_bytes=64)
         nc.vector.tensor_copy(picked_words0[:], word_table0[:].bitcast(U32).indirect(offsets[:]))
@@ -79,9 +88,6 @@ def tile_picked_modgate_linnone_p_kernel(tc, x_words, x_scales, gate, w1, offs, 
             scales=w_scales[:],
             in_=w_grouped[:].rearrange("p z n j -> p (z n j)"),
         )
-
-        picked_scales = keep.tile([P, S], U8, name="picked_scales", align_bytes=64)
-        nc.vector.tensor_copy(picked_scales[:], scale_table[:].indirect(offsets[:]))
 
         per_bank = BANK // P
         picked_gate = keep.tile([P, S], F32, name="picked_gate", align_bytes=64)

@@ -33,6 +33,12 @@ def tile_picked_modgate_linnone_p_kernel(tc, x_words, x_scales, gate, w1, offs, 
         def entries(lo, hi):
             return offsets[:, lo // LIST_COLS : hi // LIST_COLS]
 
+        zero = keep.tile([P, 1], F32, name="zero")
+        nc.vector.memset(zero[:], 0.0)
+        identity = keep.tile([P, P], F32, name="identity")
+        nc.vector.memset(identity[:], 0.0)
+        make_identity(nc, identity[:], nomemset=True)
+
         gate_table = keep.tile([P, T], F32, name="gate_table", align_bytes=64)
         nc.sync.dma_start(gate_table[P - 1 : P, :], gate[0:1, :])
         nc.vector.memset(gate_table[0 : P - 1, :], 0.0)
@@ -45,7 +51,6 @@ def tile_picked_modgate_linnone_p_kernel(tc, x_words, x_scales, gate, w1, offs, 
             )
         nc.vector.memset(scale_table[0:96, :].bitcast(I32), 0)
         picked_scales = keep.tile([P, S], U8, name="picked_scales", align_bytes=64)
-        nc.vector.memset(picked_scales[:].bitcast(I32), 0)
 
         word_table0 = keep.tile([P, T], I32, name="word_table0", align_bytes=64)
         nc.sync.dma_start(word_table0[:], x_words[0].rearrange("p t r -> p (t r)").bitcast(I32))
@@ -57,11 +62,6 @@ def tile_picked_modgate_linnone_p_kernel(tc, x_words, x_scales, gate, w1, offs, 
         word_table1 = keep.tile([P, T], I32, name="word_table1", align_bytes=64)
         nc.sync.dma_start(word_table1[:], x_words[1].rearrange("p t r -> p (t r)").bitcast(I32))
 
-        identity = keep.tile([P, P], F32, name="identity")
-        make_identity(nc, identity[:])
-
-        zero = keep.tile([P, 1], F32, name="zero")
-        nc.gpsimd.memset(zero[:], 0.0)
         window = keep.tile([P, T], F32, name="window", align_bytes=64)
         nc.scalar.copy(window[:], zero[:].to_broadcast([P, T]))
 
@@ -103,21 +103,32 @@ def tile_picked_modgate_linnone_p_kernel(tc, x_words, x_scales, gate, w1, offs, 
                 nc.tensor.transpose(spread[:, c, :], gate_col[:, c : c + 1].to_broadcast([P, P]), identity[:])
             nc.scalar.copy(picked_gate[:, h * BANK : (h + 1) * BANK], spread[:].rearrange("p c n -> p (c n)"))
 
+        def mx_pass(acc, z, words, lo, hi):
+            nc.tensor.matmul_mx(
+                out=acc[:],
+                lhsT=w_codes[:, z * N : (z + 1) * N].bitcast(FP8X4),
+                lhsT_scale=w_scales[:, z * N : (z + 1) * N],
+                rhs=words.bitcast(FP8X4),
+                rhs_scale=picked_scales[4 * z : P, lo:hi],
+                start=(z == 0),
+                stop=(z == PASSES - 1),
+            )
+
+        pieces = [(0, 256), (256, 768), (768, S)]
+        accs = [psum.tile([P, hi - lo], F32, name=f"acc{lo}") for lo, hi in pieces]
+
+        def first_pass(i):
+            lo, hi = pieces[i]
+            mx_pass(accs[i], 0, picked_words0[:, lo:hi], lo, hi)
+
+        first_pass(0)
         y = keep.tile([P, S], F32, name="y", align_bytes=64)
-        for i, (lo, hi) in enumerate([(0, 256), (256, 768), (768, 1024)]):
-            picked_words1 = keep.tile([P, hi - lo], U32, name=f"picked_words1_{i}", align_bytes=64)
+        for i, (acc, (lo, hi)) in enumerate(zip(accs, pieces)):
+            if i + 1 < len(pieces):
+                first_pass(i + 1)
+            picked_words1 = keep.tile([P, hi - lo], U32, name=f"picked_words1_{lo}", align_bytes=64)
             nc.vector.tensor_copy(picked_words1[:], word_table1[:].bitcast(U32).indirect(entries(lo, hi)))
-            acc = psum.tile([P, hi - lo], F32, name=f"acc{i}")
-            for z, words in enumerate((picked_words0[:, lo:hi], picked_words1[:])):
-                nc.tensor.matmul_mx(
-                    out=acc[:],
-                    lhsT=w_codes[:, z * N : (z + 1) * N].bitcast(FP8X4),
-                    lhsT_scale=w_scales[:, z * N : (z + 1) * N],
-                    rhs=words.bitcast(FP8X4),
-                    rhs_scale=picked_scales[4 * z : P, lo:hi],
-                    start=(z == 0),
-                    stop=(z == PASSES - 1),
-                )
+            mx_pass(acc, 1, picked_words1[:], lo, hi)
             nc.scalar.copy(y[:, lo:hi], acc[:])
 
         for lo, hi in [(0, 256), (256, S)]:

@@ -13,12 +13,18 @@ U32 = mybir.dt.uint32
 U16 = mybir.dt.uint16
 U8 = mybir.dt.uint8
 FP8X4 = mybir.dt.float8_e4m3fn_x4
+ALU = mybir.AluOpType
+ACT = mybir.ActivationFunctionType
 
 P = 128
 PACK = 4
 PASSES = K // (P * PACK)
 BANK = 512
 LIST_COLS = 16
+STRIP = T // P
+SIGNS = 2
+LN_LOW, LN_HIGH = 2.0**-63, 2.0**63
+HALF = S // 2
 
 
 def tile_picked_modgate_linnone_p_kernel(tc, x_words, x_scales, gate, w1, offs, out):
@@ -27,17 +33,20 @@ def tile_picked_modgate_linnone_p_kernel(tc, x_words, x_scales, gate, w1, offs, 
         keep = ctx.enter_context(tc.tile_pool(name="keep", bufs=1))
         psum = ctx.enter_context(tc.psum_pool(name="psum", bufs=1))
 
+        strips = keep.tile([P, STRIP], F32, name="strips", tag="strips_then_window", align_bytes=64)
+        nc.sync.dma_start(strips[:], gate[0, :].rearrange("(p c) -> p c", c=STRIP))
+
         offsets = keep.tile([P, S // LIST_COLS], U16, name="offsets")
         nc.sync.dma_start(offsets[:], offs)
 
         def entries(lo, hi):
             return offsets[:, lo // LIST_COLS : hi // LIST_COLS]
 
-        zero = keep.tile([P, 1], F32, name="zero")
-        nc.vector.memset(zero[:], 0.0)
         identity = keep.tile([P, P], F32, name="identity")
         nc.vector.memset(identity[:], 0.0)
         make_identity(nc, identity[:], nomemset=True)
+        logs = keep.tile([P, SIGNS * STRIP + P], F32, name="logs")
+        nc.vector.memset(logs[:, SIGNS * STRIP :], 0.0)
 
         gate_table = keep.tile([P, T], F32, name="gate_table", align_bytes=64)
         nc.sync.dma_start(gate_table[P - 1 : P, :], gate[0:1, :])
@@ -50,37 +59,40 @@ def tile_picked_modgate_linnone_p_kernel(tc, x_words, x_scales, gate, w1, offs, 
                 x_scales[z].bitcast(I32).rearrange("(q r) c -> r q c", r=4),
             )
         nc.vector.memset(scale_table[0:96, :].bitcast(I32), 0)
-        picked_scales = keep.tile([P, S], U8, name="picked_scales", align_bytes=64)
 
-        word_table0 = keep.tile([P, T], I32, name="word_table0", align_bytes=64)
-        nc.sync.dma_start(word_table0[:], x_words[0].rearrange("p t r -> p (t r)").bitcast(I32))
         w_raw = keep.tile([P, PASSES, PACK, N], F32, name="w_raw")
         nc.sync.dma_start(
             w_raw[:].rearrange("p z j n -> p z (j n)"),
             w1.rearrange("(z p j) n -> p z (j n)", z=PASSES, j=PACK),
         )
+        word_table0 = keep.tile([P, T], I32, name="word_table0", align_bytes=64)
+        nc.sync.dma_start(word_table0[:], x_words[0].rearrange("p t r -> p (t r)").bitcast(I32))
         word_table1 = keep.tile([P, T], I32, name="word_table1", align_bytes=64)
         nc.sync.dma_start(word_table1[:], x_words[1].rearrange("p t r -> p (t r)").bitcast(I32))
 
-        window = keep.tile([P, T], F32, name="window", align_bytes=64)
-        nc.scalar.copy(window[:], zero[:].to_broadcast([P, T]))
+        parts = keep.tile([P, SIGNS, STRIP], F32, name="parts")
+        nc.gpsimd.tensor_scalar(parts[:, 0, :], strips[:], LN_LOW, LN_HIGH, ALU.max, ALU.min)
+        nc.gpsimd.tensor_scalar(parts[:, 1, :], strips[:], -LN_LOW, -LN_HIGH, ALU.min, ALU.max)
+        window = keep.tile([P, T], F32, name="window", tag="strips_then_window", align_bytes=64)
+        nc.gpsimd.memset(window[:], 0.0)
+        by_sign = logs[:, 0 : SIGNS * STRIP].rearrange("p (c s) -> p s c", s=SIGNS)
+        for s, sign in enumerate((1.0, -1.0)):
+            nc.scalar.activation(by_sign[:, s, :], parts[:, s, :], ACT.Ln, scale=sign)
 
-        gate_row = keep.tile([P, S], F32, name="gate_row", align_bytes=64)
-        nc.vector.tensor_copy(gate_row[:], gate_table[:].indirect(offsets[:]))
+        gate_row = keep.tile([P, HALF], F32, name="gate_row", align_bytes=64)
+        nc.vector.tensor_copy(gate_row[:], gate_table[:].indirect(entries(0, HALF)))
 
         picked_rows = keep.tile([P, S], U8, name="picked_rows", align_bytes=64)
         nc.vector.tensor_copy(picked_rows[:], scale_table[:].indirect(offsets[:]))
+        picked_scales = keep.tile([P, S], U8, name="picked_scales", align_bytes=64)
         for q in range(4):
             nc.sync.dma_start(
                 picked_scales[32 * q : 32 * q + 4 * PASSES, :].bitcast(I32),
                 picked_rows[96 + q : P : 4, :].bitcast(I32),
             )
 
-        picked_words0 = keep.tile([P, S], U32, name="picked_words0", align_bytes=64)
-        nc.vector.tensor_copy(picked_words0[:], word_table0[:].bitcast(U32).indirect(offsets[:]))
-
-        w_grouped = keep.tile([P, PASSES, N, PACK], BF16, name="w_grouped", align_bytes=64)
-        nc.scalar.copy(w_grouped[:], w_raw[:].rearrange("p z j n -> p z n j"))
+        w_grouped = keep.tile([P, PASSES, N, PACK], BF16, name="w_grouped", tag="grouped_then_words", align_bytes=64)
+        nc.gpsimd.tensor_scalar(w_grouped[:], w_raw[:].rearrange("p z j n -> p z n j"), 1.0, 0.0, ALU.mult, ALU.add)
         w_codes = keep.tile([P, PASSES * N], U32, name="w_codes", align_bytes=64)
         w_scales = keep.tile([P, PASSES * N], U8, name="w_scales", align_bytes=64)
         nc.vector.quantize_mx(
@@ -90,18 +102,41 @@ def tile_picked_modgate_linnone_p_kernel(tc, x_words, x_scales, gate, w1, offs, 
         )
 
         per_bank = BANK // P
+        log_table = keep.tile([P, T], F32, name="log_table", align_bytes=64)
+        for b in range(T // BANK):
+            rows = psum.tile([P, per_bank, P], F32, name=f"rows{b}", tag=f"bank{b}")
+            for i in range(per_bank):
+                c = b * per_bank + i
+                nc.tensor.transpose(rows[:, i, :], logs[:, SIGNS * c : SIGNS * c + P], identity[:])
+            nc.scalar.copy(
+                log_table[:].rearrange("p (t c) -> p t c", c=STRIP)[:, :, b * per_bank : (b + 1) * per_bank],
+                rows[:].rearrange("p i t -> p t i"),
+            )
+
+        picked_words0 = keep.tile([P, S], U32, name="picked_words0", align_bytes=64)
+        nc.vector.tensor_copy(picked_words0[:], word_table0[:].bitcast(U32).indirect(offsets[:]))
+
         picked_gate = keep.tile([P, S], F32, name="picked_gate", align_bytes=64)
-        for h in range(S // BANK):
-            turned = psum.tile([P, per_bank, P], F32, name=f"turned{h}")
+
+        def turn(row, bank):
+            turned = psum.tile([P, per_bank, P], F32, name=f"turned_{bank}", tag=bank)
             for c in range(per_bank):
-                lo = h * BANK + c * P
-                nc.tensor.transpose(turned[:, c, :], gate_row[:, lo : lo + P], identity[:])
-            gate_col = keep.tile([P, per_bank], F32, name=f"gate_col{h}")
-            nc.scalar.copy(gate_col[:], turned[:, :, P - 1])
-            spread = psum.tile([P, per_bank, P], F32, name=f"spread{h}")
+                nc.tensor.transpose(turned[:, c, :], row[:, c * P : (c + 1) * P], identity[:])
+            return turned
+
+        def spread(cols, lo, bank):
+            spread = psum.tile([P, per_bank, P], F32, name=f"spread{lo}", tag=bank)
             for c in range(per_bank):
-                nc.tensor.transpose(spread[:, c, :], gate_col[:, c : c + 1].to_broadcast([P, P]), identity[:])
-            nc.scalar.copy(picked_gate[:, h * BANK : (h + 1) * BANK], spread[:].rearrange("p c n -> p (c n)"))
+                nc.tensor.transpose(spread[:, c, :], cols[:, c : c + 1].to_broadcast([P, P]), identity[:])
+            nc.scalar.copy(picked_gate[:, lo : lo + HALF], spread[:].rearrange("p c n -> p (c n)"))
+
+        turned = turn(gate_row, "bank0")
+        gate_cols = keep.tile([P, per_bank], F32, name="gate_cols")
+        nc.scalar.copy(gate_cols[:], turned[:, :, P - 1])
+        spread(gate_cols, 0, "bank5")
+
+        picked_parts = keep.tile([P, HALF], F32, name="picked_parts", align_bytes=64)
+        nc.scalar.activation(picked_parts[:], log_table[:].indirect(entries(HALF, S)), ACT.Exp)
 
         def mx_pass(acc, z, words, lo, hi):
             nc.tensor.matmul_mx(
@@ -114,25 +149,35 @@ def tile_picked_modgate_linnone_p_kernel(tc, x_words, x_scales, gate, w1, offs, 
                 stop=(z == PASSES - 1),
             )
 
-        pieces = [(0, 256), (256, 768), (768, S)]
-        accs = [psum.tile([P, hi - lo], F32, name=f"acc{lo}") for lo, hi in pieces]
-
-        def first_pass(i):
-            lo, hi = pieces[i]
-            mx_pass(accs[i], 0, picked_words0[:, lo:hi], lo, hi)
-
-        first_pass(0)
         y = keep.tile([P, S], F32, name="y", align_bytes=64)
-        for i, (acc, (lo, hi)) in enumerate(zip(accs, pieces)):
-            if i + 1 < len(pieces):
-                first_pass(i + 1)
-            picked_words1 = keep.tile([P, hi - lo], U32, name=f"picked_words1_{lo}", align_bytes=64)
-            nc.vector.tensor_copy(picked_words1[:], word_table1[:].bitcast(U32).indirect(entries(lo, hi)))
-            mx_pass(acc, 1, picked_words1[:], lo, hi)
+        picked_words1 = keep.tile([P, S], U32, name="picked_words1", tag="grouped_then_words", align_bytes=64)
+
+        def first_pass(lo, hi, bank):
+            acc = psum.tile([P, hi - lo], F32, name=f"acc{lo}", tag=bank)
+            mx_pass(acc, 0, picked_words0[:, lo:hi], lo, hi)
+            return acc
+
+        def last_pass(acc, lo, hi):
+            nc.vector.tensor_copy(picked_words1[:, lo:hi], word_table1[:].bitcast(U32).indirect(entries(lo, hi)))
+            mx_pass(acc, 1, picked_words1[:, lo:hi], lo, hi)
             nc.scalar.copy(y[:, lo:hi], acc[:])
 
-        for lo, hi in [(0, 256), (256, S)]:
+        early = [(0, 256), (256, HALF)]
+        accs = [first_pass(lo, hi, f"bank{i + 1}") for i, (lo, hi) in enumerate(early)]
+        for acc, (lo, hi) in zip(accs, early):
+            last_pass(acc, lo, hi)
+
+        turned = turn(picked_parts, "bank1")
+        both = keep.tile([P, per_bank, SIGNS], F32, name="both")
+        nc.scalar.copy(both[:], turned[:, :, 0:SIGNS])
+        late_cols = keep.tile([P, per_bank], F32, name="late_cols")
+        nc.gpsimd.tensor_tensor(late_cols[:], both[:, :, 0], both[:, :, 1], ALU.subtract)
+        acc = first_pass(HALF, S, "bank1")
+        last_pass(acc, HALF, S)
+        spread(late_cols, HALF, "bank7")
+
+        for lo, hi in [(0, HALF), (HALF, S)]:
             nc.vector.tensor_tensor(
-                window[:].indirect(entries(lo, hi)), y[:, lo:hi], picked_gate[:, lo:hi], mybir.AluOpType.mult
+                window[:].indirect(entries(lo, hi)), y[:, lo:hi], picked_gate[:, lo:hi], ALU.mult
             )
         nc.sync.dma_start(out, window[:])

@@ -171,7 +171,10 @@ def tile_picked_modgate_linnone_p_kernel(tc, x_words, x_scales, gate, w1, offs, 
         both = keep.tile([P, per_bank, SIGNS], F32, name="both")
         nc.scalar.copy(both[:], turned[:, :, 0:SIGNS])
         late_cols = keep.tile([P, per_bank], F32, name="late_cols")
-        nc.gpsimd.tensor_tensor(late_cols[:], both[:, :, 0], both[:, :, 1], ALU.subtract)
+        for c in range(per_bank):
+            nc.scalar.activation(
+                late_cols[:, c : c + 1], both[:, c, 1:2], ACT.Identity, bias=both[:, c, 0:1], scale=-1.0
+            )
         acc = first_pass(HALF, S, "bank1")
         last_pass(acc, HALF, S)
         spread(late_cols, HALF, "bank7")

@@ -70,14 +70,17 @@ def tile_picked_modgate_linnone_p_kernel(tc, x_words, x_scales, gate, w1, offs, 
         word_table1 = keep.tile([P, T], I32, name="word_table1", align_bytes=64)
         nc.sync.dma_start(word_table1[:], x_words[1].rearrange("p t r -> p (t r)").bitcast(I32))
 
-        parts = keep.tile([P, SIGNS, STRIP], F32, name="parts")
-        nc.gpsimd.tensor_scalar(parts[:, 0, :], strips[:], LN_LOW, LN_HIGH, ALU.max, ALU.min)
-        nc.gpsimd.tensor_scalar(parts[:, 1, :], strips[:], -LN_LOW, -LN_HIGH, ALU.min, ALU.max)
+        parts = keep.tile([P, SIGNS, STRIP], F32, name="parts", tag="grouped_then_words", align_bytes=64)
+        nc.vector.tensor_scalar(parts[:, 0, :], strips[:], LN_LOW, LN_HIGH, ALU.max, ALU.min)
+        nc.vector.tensor_scalar(parts[:, 1, :], strips[:], -LN_LOW, -LN_HIGH, ALU.min, ALU.max)
         window = keep.tile([P, T], F32, name="window", tag="strips_then_window", align_bytes=64)
         nc.gpsimd.memset(window[:], 0.0)
         by_sign = logs[:, 0 : SIGNS * STRIP].rearrange("p (c s) -> p s c", s=SIGNS)
         for s, sign in enumerate((1.0, -1.0)):
             nc.scalar.activation(by_sign[:, s, :], parts[:, s, :], ACT.Ln, scale=sign)
+
+        warm = keep.tile([P, 1], F32, name="warm")
+        nc.scalar.activation(warm[:], logs[:, 1:2], ACT.Exp)
 
         gate_row = keep.tile([P, HALF], F32, name="gate_row", align_bytes=64)
         nc.vector.tensor_copy(gate_row[:], gate_table[:].indirect(entries(0, HALF)))
@@ -92,7 +95,7 @@ def tile_picked_modgate_linnone_p_kernel(tc, x_words, x_scales, gate, w1, offs, 
             )
 
         w_grouped = keep.tile([P, PASSES, N, PACK], BF16, name="w_grouped", tag="grouped_then_words", align_bytes=64)
-        nc.gpsimd.tensor_scalar(w_grouped[:], w_raw[:].rearrange("p z j n -> p z n j"), 1.0, 0.0, ALU.mult, ALU.add)
+        nc.scalar.copy(w_grouped[:], w_raw[:].rearrange("p z j n -> p z n j"))
         w_codes = keep.tile([P, PASSES * N], U32, name="w_codes", align_bytes=64)
         w_scales = keep.tile([P, PASSES * N], U8, name="w_scales", align_bytes=64)
         nc.vector.quantize_mx(

@@ -22,8 +22,9 @@ PASSES = K // (P * PACK)
 BANK = 512
 LIST_COLS = 16
 STRIP = T // P
-SIGNS = 2
-LN_LOW, LN_HIGH = 2.0**-63, 2.0**63
+PARTS = 4
+SMALLEST = 2.0**-126
+UP, DOWN = 2.0**63, 2.0**-64
 HALF = S // 2
 
 
@@ -45,8 +46,8 @@ def tile_picked_modgate_linnone_p_kernel(tc, x_words, x_scales, gate, w1, offs, 
         identity = keep.tile([P, P], F32, name="identity")
         nc.vector.memset(identity[:], 0.0)
         make_identity(nc, identity[:], nomemset=True)
-        logs = keep.tile([P, SIGNS * STRIP + P], F32, name="logs")
-        nc.vector.memset(logs[:, SIGNS * STRIP :], 0.0)
+        logs = keep.tile([P, PARTS * STRIP + P], F32, name="logs")
+        nc.vector.memset(logs[:, PARTS * STRIP :], 0.0)
 
         gate_table = keep.tile([P, T], F32, name="gate_table", align_bytes=64)
         nc.sync.dma_start(gate_table[P - 1 : P, :], gate[0:1, :])
@@ -60,27 +61,28 @@ def tile_picked_modgate_linnone_p_kernel(tc, x_words, x_scales, gate, w1, offs, 
             )
         nc.vector.memset(scale_table[0:96, :].bitcast(I32), 0)
 
-        w_raw = keep.tile([P, PASSES, PACK, N], F32, name="w_raw")
-        nc.sync.dma_start(
-            w_raw[:].rearrange("p z j n -> p z (j n)"),
-            w1.rearrange("(z p j) n -> p z (j n)", z=PASSES, j=PACK),
-        )
-        word_table0 = keep.tile([P, T], I32, name="word_table0", align_bytes=64)
-        nc.sync.dma_start(word_table0[:], x_words[0].rearrange("p t r -> p (t r)").bitcast(I32))
-        word_table1 = keep.tile([P, T], I32, name="word_table1", align_bytes=64)
-        nc.sync.dma_start(word_table1[:], x_words[1].rearrange("p t r -> p (t r)").bitcast(I32))
+        w_rows = w1.rearrange("(z p j) n -> z p (j n)", z=PASSES, j=PACK)
+        w_raw, word_tables = [], []
+        for z in range(PASSES):
+            w_raw.append(keep.tile([P, PACK, N], F32, name=f"w_raw{z}"))
+            nc.sync.dma_start(w_raw[z][:].rearrange("p j n -> p (j n)"), w_rows[z])
+            word_tables.append(keep.tile([P, T], I32, name=f"word_table{z}", align_bytes=64))
+            nc.sync.dma_start(word_tables[z][:], x_words[z].rearrange("p t r -> p (t r)").bitcast(I32))
 
-        parts = keep.tile([P, SIGNS, STRIP], F32, name="parts", tag="grouped_then_words", align_bytes=64)
-        nc.vector.tensor_scalar(parts[:, 0, :], strips[:], LN_LOW, LN_HIGH, ALU.max, ALU.min)
-        nc.vector.tensor_scalar(parts[:, 1, :], strips[:], -LN_LOW, -LN_HIGH, ALU.min, ALU.max)
+        parts = keep.tile([P, PARTS, STRIP], F32, name="parts", tag="grouped_then_words", align_bytes=64)
+        nc.vector.tensor_scalar(parts[:, 0, :], strips[:], DOWN, DOWN, ALU.mult, ALU.max)
+        nc.vector.tensor_scalar(parts[:, 1, :], strips[:], -DOWN, DOWN, ALU.mult, ALU.max)
+        nc.vector.tensor_scalar(parts[:, 2, :], strips[:], SMALLEST, 1.0, ALU.max, ALU.min)
+        nc.vector.tensor_scalar(parts[:, 3, :], strips[:], -SMALLEST, -1.0, ALU.min, ALU.max)
         window = keep.tile([P, T], F32, name="window", tag="strips_then_window", align_bytes=64)
         nc.gpsimd.memset(window[:], 0.0)
-        by_sign = logs[:, 0 : SIGNS * STRIP].rearrange("p (c s) -> p s c", s=SIGNS)
-        for s, sign in enumerate((1.0, -1.0)):
-            nc.scalar.activation(by_sign[:, s, :], parts[:, s, :], ACT.Ln, scale=sign)
+        by_part = logs[:, 0 : PARTS * STRIP].rearrange("p (c v) -> p v c", v=PARTS)
+        nc.scalar.activation(by_part[:, 0:2, :], parts[:, 0:2, :], ACT.Ln)
+        nc.scalar.activation(by_part[:, 2, :], parts[:, 2, :], ACT.Ln, scale=UP)
+        nc.scalar.activation(by_part[:, 3, :], parts[:, 3, :], ACT.Ln, scale=-UP)
 
         warm = keep.tile([P, 1], F32, name="warm")
-        nc.scalar.activation(warm[:], logs[:, 1:2], ACT.Exp)
+        nc.scalar.activation(warm[:], logs[:, PARTS - 1 : PARTS], ACT.Exp)
 
         gate_row = keep.tile([P, HALF], F32, name="gate_row", align_bytes=64)
         nc.vector.tensor_copy(gate_row[:], gate_table[:].indirect(entries(0, HALF)))
@@ -95,7 +97,28 @@ def tile_picked_modgate_linnone_p_kernel(tc, x_words, x_scales, gate, w1, offs, 
             )
 
         w_grouped = keep.tile([P, PASSES, N, PACK], BF16, name="w_grouped", tag="grouped_then_words", align_bytes=64)
-        nc.scalar.copy(w_grouped[:], w_raw[:].rearrange("p z j n -> p z n j"))
+
+        def cast(z):
+            nc.scalar.copy(w_grouped[:, z], w_raw[z][:].rearrange("p j n -> p n j"))
+
+        per_bank = BANK // P
+        log_table = keep.tile([P, T], F32, name="log_table", align_bytes=64)
+
+        def lay_rows(b):
+            rows = psum.tile([P, per_bank, P], F32, name=f"rows{b}", tag=f"bank{b}")
+            for i in range(per_bank):
+                c = b * per_bank + i
+                nc.tensor.transpose(rows[:, i, :], logs[:, PARTS * c : PARTS * c + P], identity[:])
+            nc.scalar.copy(
+                log_table[:].rearrange("p (t c) -> p t c", c=STRIP)[:, :, b * per_bank : (b + 1) * per_bank],
+                rows[:].rearrange("p i t -> p t i"),
+            )
+
+        for z in range(PASSES):
+            cast(z)
+            lay_rows(2 * z)
+            lay_rows(2 * z + 1)
+
         w_codes = keep.tile([P, PASSES * N], U32, name="w_codes", align_bytes=64)
         w_scales = keep.tile([P, PASSES * N], U8, name="w_scales", align_bytes=64)
         nc.vector.quantize_mx(
@@ -104,20 +127,8 @@ def tile_picked_modgate_linnone_p_kernel(tc, x_words, x_scales, gate, w1, offs, 
             in_=w_grouped[:].rearrange("p z n j -> p (z n j)"),
         )
 
-        per_bank = BANK // P
-        log_table = keep.tile([P, T], F32, name="log_table", align_bytes=64)
-        for b in range(T // BANK):
-            rows = psum.tile([P, per_bank, P], F32, name=f"rows{b}", tag=f"bank{b}")
-            for i in range(per_bank):
-                c = b * per_bank + i
-                nc.tensor.transpose(rows[:, i, :], logs[:, SIGNS * c : SIGNS * c + P], identity[:])
-            nc.scalar.copy(
-                log_table[:].rearrange("p (t c) -> p t c", c=STRIP)[:, :, b * per_bank : (b + 1) * per_bank],
-                rows[:].rearrange("p i t -> p t i"),
-            )
-
         picked_words0 = keep.tile([P, S], U32, name="picked_words0", align_bytes=64)
-        nc.vector.tensor_copy(picked_words0[:], word_table0[:].bitcast(U32).indirect(offsets[:]))
+        nc.vector.tensor_copy(picked_words0[:], word_tables[0][:].bitcast(U32).indirect(offsets[:]))
 
         picked_gate = keep.tile([P, S], F32, name="picked_gate", align_bytes=64)
 
@@ -161,7 +172,7 @@ def tile_picked_modgate_linnone_p_kernel(tc, x_words, x_scales, gate, w1, offs, 
             return acc
 
         def last_pass(acc, lo, hi):
-            nc.vector.tensor_copy(picked_words1[:, lo:hi], word_table1[:].bitcast(U32).indirect(entries(lo, hi)))
+            nc.vector.tensor_copy(picked_words1[:, lo:hi], word_tables[1][:].bitcast(U32).indirect(entries(lo, hi)))
             mx_pass(acc, 1, picked_words1[:, lo:hi], lo, hi)
             nc.scalar.copy(y[:, lo:hi], acc[:])
 
@@ -171,15 +182,15 @@ def tile_picked_modgate_linnone_p_kernel(tc, x_words, x_scales, gate, w1, offs, 
             last_pass(acc, lo, hi)
 
         turned = turn(picked_parts, "bank1")
-        both = keep.tile([P, per_bank, SIGNS], F32, name="both")
-        nc.scalar.copy(both[:], turned[:, :, 0:SIGNS])
+        terms = keep.tile([P, per_bank, PARTS], F32, name="terms")
+        for v, back in enumerate((1 / DOWN, -1 / DOWN, 1 / UP, -1 / UP)):
+            nc.scalar.activation(terms[:, :, v], turned[:, :, v], ACT.Copy, scale=back)
         late_cols = keep.tile([P, per_bank], F32, name="late_cols")
+        summed = keep.tile([P, per_bank, PARTS], F32, name="summed")
         for c in range(per_bank):
-            nc.scalar.activation(
-                late_cols[:, c : c + 1], both[:, c, 1:2], ACT.Identity, bias=both[:, c, 0:1], scale=-1.0
-            )
-        acc = first_pass(HALF, S, "bank1")
-        last_pass(acc, HALF, S)
+            nc.scalar.activation(summed[:, c, :], terms[:, c, :], ACT.Copy, accum_out=late_cols[:, c : c + 1])
+        last_pass(first_pass(HALF, 768, "bank2"), HALF, 768)
+        last_pass(first_pass(768, S, "bank1"), 768, S)
         spread(late_cols, HALF, "bank7")
 
         for lo, hi in [(0, HALF), (HALF, S)]:

@@ -44,10 +44,9 @@ def tile_picked_modgate_linnone_p_kernel(tc, x_words, x_scales, gate, w1, offs, 
             return offsets[:, lo // LIST_COLS : hi // LIST_COLS]
 
         identity = keep.tile([P, P], F32, name="identity")
-        nc.vector.memset(identity[:], 0.0)
-        make_identity(nc, identity[:], nomemset=True)
+        make_identity(nc, identity[:])
         logs = keep.tile([P, PARTS * STRIP + P], F32, name="logs")
-        nc.vector.memset(logs[:, PARTS * STRIP :], 0.0)
+        nc.gpsimd.memset(logs[:, PARTS * STRIP :], 0.0)
 
         gate_table = keep.tile([P, T], F32, name="gate_table", align_bytes=64)
         nc.sync.dma_start(gate_table[P - 1 : P, :], gate[0:1, :])
@@ -171,15 +170,19 @@ def tile_picked_modgate_linnone_p_kernel(tc, x_words, x_scales, gate, w1, offs, 
             mx_pass(acc, 0, picked_words0[:, lo:hi], lo, hi)
             return acc
 
-        def last_pass(acc, lo, hi):
+        def gather_words1(lo, hi):
             nc.vector.tensor_copy(picked_words1[:, lo:hi], word_tables[1][:].bitcast(U32).indirect(entries(lo, hi)))
+
+        def last_pass(acc, lo, hi):
             mx_pass(acc, 1, picked_words1[:, lo:hi], lo, hi)
             nc.scalar.copy(y[:, lo:hi], acc[:])
 
         early = [(0, 256), (256, HALF)]
         accs = [first_pass(lo, hi, f"bank{i + 1}") for i, (lo, hi) in enumerate(early)]
         for acc, (lo, hi) in zip(accs, early):
+            gather_words1(lo, hi)
             last_pass(acc, lo, hi)
+        gather_words1(HALF, S)
 
         turned = turn(picked_parts, "bank1")
         terms = keep.tile([P, per_bank, PARTS], F32, name="terms")

@@ -86,7 +86,7 @@ def tile_picked_modgate_linnone_p_kernel(tc, x_words, x_scales, gate, w1, offs, 
         gate_row = keep.tile([P, HALF], F32, name="gate_row", align_bytes=64)
         nc.vector.tensor_copy(gate_row[:], gate_table[:].indirect(entries(0, HALF)))
 
-        picked_rows = keep.tile([P, S], U8, name="picked_rows", align_bytes=64)
+        picked_rows = keep.tile([P, S], U8, name="picked_rows", tag="rows_then_gate", align_bytes=64)
         nc.vector.tensor_copy(picked_rows[:], scale_table[:].indirect(offsets[:]))
         picked_scales = keep.tile([P, S], U8, name="picked_scales", align_bytes=64)
         for q in range(4):
@@ -129,7 +129,7 @@ def tile_picked_modgate_linnone_p_kernel(tc, x_words, x_scales, gate, w1, offs, 
         picked_words0 = keep.tile([P, S], U32, name="picked_words0", align_bytes=64)
         nc.vector.tensor_copy(picked_words0[:], word_tables[0][:].bitcast(U32).indirect(offsets[:]))
 
-        picked_gate = keep.tile([P, S], F32, name="picked_gate", align_bytes=64)
+        picked_gate = keep.tile([P, S], F32, name="picked_gate", tag="rows_then_gate", align_bytes=64)
 
         def turn(row, bank):
             turned = psum.tile([P, per_bank, P], F32, name=f"turned_{bank}", tag=bank)
@@ -184,7 +184,7 @@ def tile_picked_modgate_linnone_p_kernel(tc, x_words, x_scales, gate, w1, offs, 
             last_pass(acc, lo, hi)
         gather_words1(HALF, S)
 
-        turned = turn(picked_parts, "bank1")
+        turned = turn(picked_parts, "bank5")
         terms = keep.tile([P, per_bank, PARTS], F32, name="terms")
         for v, back in enumerate((1 / DOWN, -1 / DOWN, 1 / UP, -1 / UP)):
             nc.scalar.activation(terms[:, :, v], turned[:, :, v], ACT.Copy, scale=back)
@@ -192,8 +192,8 @@ def tile_picked_modgate_linnone_p_kernel(tc, x_words, x_scales, gate, w1, offs, 
         summed = keep.tile([P, per_bank, PARTS], F32, name="summed")
         for c in range(per_bank):
             nc.scalar.activation(summed[:, c, :], terms[:, c, :], ACT.Copy, accum_out=late_cols[:, c : c + 1])
-        last_pass(first_pass(HALF, 768, "bank2"), HALF, 768)
-        last_pass(first_pass(768, S, "bank1"), 768, S)
+        last_pass(first_pass(HALF, 768, "bank1"), HALF, 768)
+        last_pass(first_pass(768, S, "bank2"), 768, S)
         spread(late_cols, HALF, "bank7")
 
         for lo, hi in [(0, HALF), (HALF, S)]:

@@ -60,11 +60,13 @@ def tile_picked_modgate_linnone_p_kernel(tc, x_words, x_scales, gate, w1, offs, 
             )
         nc.vector.memset(scale_table[0:96, :].bitcast(I32), 0)
 
-        w_rows = w1.rearrange("(z p j) n -> z p (j n)", z=PASSES, j=PACK)
-        w_raw, word_tables = [], []
+        w_raw = keep.tile([P, PASSES, PACK, N], F32, name="w_raw")
+        nc.sync.dma_start(
+            w_raw[:].rearrange("p z j n -> p z (j n)"),
+            w1.rearrange("(z p j) n -> p z (j n)", z=PASSES, j=PACK),
+        )
+        word_tables = []
         for z in range(PASSES):
-            w_raw.append(keep.tile([P, PACK, N], F32, name=f"w_raw{z}"))
-            nc.sync.dma_start(w_raw[z][:].rearrange("p j n -> p (j n)"), w_rows[z])
             word_tables.append(keep.tile([P, T], I32, name=f"word_table{z}", align_bytes=64))
             nc.sync.dma_start(word_tables[z][:], x_words[z].rearrange("p t r -> p (t r)").bitcast(I32))
 
@@ -96,9 +98,10 @@ def tile_picked_modgate_linnone_p_kernel(tc, x_words, x_scales, gate, w1, offs, 
             )
 
         w_grouped = keep.tile([P, PASSES, N, PACK], BF16, name="w_grouped", tag="grouped_then_words", align_bytes=64)
-
-        def cast(z):
-            nc.scalar.copy(w_grouped[:, z], w_raw[z][:].rearrange("p j n -> p n j"))
+        nc.scalar.copy(
+            w_grouped[:].rearrange("p z (c i) j -> p z c j i", i=PACK),
+            w_raw[:].rearrange("p z j (c i) -> p z c j i", i=PACK),
+        )
 
         per_bank = BANK // P
         log_table = keep.tile([P, T], F32, name="log_table", align_bytes=64)
@@ -113,10 +116,8 @@ def tile_picked_modgate_linnone_p_kernel(tc, x_words, x_scales, gate, w1, offs, 
                 rows[:].rearrange("p i t -> p t i"),
             )
 
-        for z in range(PASSES):
-            cast(z)
-            lay_rows(2 * z)
-            lay_rows(2 * z + 1)
+        for b in range(T // BANK):
+            lay_rows(b)
 
         w_codes = keep.tile([P, PASSES * N], U32, name="w_codes", align_bytes=64)
         w_scales = keep.tile([P, PASSES * N], U8, name="w_scales", align_bytes=64)

@@ -21,11 +21,10 @@ PACK = 4
 PASSES = K // (P * PACK)
 BANK = 512
 LIST_COLS = 16
-STRIP = T // P
-PARTS = 4
-SMALLEST = 2.0**-126
-UP, DOWN = 2.0**63, 2.0**-64
 HALF = S // 2
+PIECES = [(0, 256), (256, 640), (640, S)]
+STORE = 512
+HEAD = 512
 
 
 def tile_picked_modgate_linnone_p_kernel(tc, x_words, x_scales, gate, w1, offs, out):
@@ -34,23 +33,11 @@ def tile_picked_modgate_linnone_p_kernel(tc, x_words, x_scales, gate, w1, offs, 
         keep = ctx.enter_context(tc.tile_pool(name="keep", bufs=1))
         psum = ctx.enter_context(tc.psum_pool(name="psum", bufs=1))
 
-        strips = keep.tile([P, STRIP], F32, name="strips", tag="strips_then_window", align_bytes=64)
-        nc.sync.dma_start(strips[:], gate[0, :].rearrange("(p c) -> p c", c=STRIP))
-
         offsets = keep.tile([P, S // LIST_COLS], U16, name="offsets")
         nc.sync.dma_start(offsets[:], offs)
 
         def entries(lo, hi):
             return offsets[:, lo // LIST_COLS : hi // LIST_COLS]
-
-        identity = keep.tile([P, P], F32, name="identity")
-        make_identity(nc, identity[:])
-        logs = keep.tile([P, PARTS * STRIP + P], F32, name="logs")
-        nc.gpsimd.memset(logs[:, PARTS * STRIP :], 0.0)
-
-        gate_table = keep.tile([P, T], F32, name="gate_table", align_bytes=64)
-        nc.sync.dma_start(gate_table[P - 1 : P, :], gate[0:1, :])
-        nc.vector.memset(gate_table[0 : P - 1, :], 0.0)
 
         scale_table = keep.tile([P, T], U8, name="scale_table", align_bytes=64)
         for z in range(PASSES):
@@ -60,42 +47,61 @@ def tile_picked_modgate_linnone_p_kernel(tc, x_words, x_scales, gate, w1, offs, 
             )
         nc.vector.memset(scale_table[0:96, :].bitcast(I32), 0)
 
+        identity = keep.tile([P, P], F32, name="identity")
+        make_identity(nc, identity[:])
+
+        gate_table = keep.tile([P, T], F32, name="gate_table", tag="gate_then_scales", align_bytes=64)
+        nc.sync.dma_start(gate_table[P - 1 : P, :], gate[0:1, :])
+        nc.gpsimd.memset(gate_table[0 : P - 1, :], 0.0)
+
+        word_tables = [keep.tile([P, T], I32, name=f"word_table{z}", align_bytes=64) for z in range(PASSES)]
         w_raw = keep.tile([P, PASSES, PACK, N], F32, name="w_raw")
+
+        def load_words(z):
+            nc.sync.dma_start(word_tables[z][:], x_words[z].rearrange("p t r -> p (t r)").bitcast(I32))
+
+        load_words(0)
         nc.sync.dma_start(
             w_raw[:].rearrange("p z j n -> p z (j n)"),
             w1.rearrange("(z p j) n -> p z (j n)", z=PASSES, j=PACK),
         )
-        word_tables = []
-        for z in range(PASSES):
-            word_tables.append(keep.tile([P, T], I32, name=f"word_table{z}", align_bytes=64))
-            nc.sync.dma_start(word_tables[z][:], x_words[z].rearrange("p t r -> p (t r)").bitcast(I32))
+        load_words(1)
 
-        parts = keep.tile([P, PARTS, STRIP], F32, name="parts", tag="grouped_then_words", align_bytes=64)
-        nc.vector.tensor_scalar(parts[:, 0, :], strips[:], DOWN, DOWN, ALU.mult, ALU.max)
-        nc.vector.tensor_scalar(parts[:, 1, :], strips[:], -DOWN, DOWN, ALU.mult, ALU.max)
-        nc.vector.tensor_scalar(parts[:, 2, :], strips[:], SMALLEST, 1.0, ALU.max, ALU.min)
-        nc.vector.tensor_scalar(parts[:, 3, :], strips[:], -SMALLEST, -1.0, ALU.min, ALU.max)
-        window = keep.tile([P, T], F32, name="window", tag="strips_then_window", align_bytes=64)
-        nc.gpsimd.memset(window[:], 0.0)
-        by_part = logs[:, 0 : PARTS * STRIP].rearrange("p (c v) -> p v c", v=PARTS)
-        nc.scalar.activation(by_part[:, 0:2, :], parts[:, 0:2, :], ACT.Ln)
-        nc.scalar.activation(by_part[:, 2, :], parts[:, 2, :], ACT.Ln, scale=UP)
-        nc.scalar.activation(by_part[:, 3, :], parts[:, 3, :], ACT.Ln, scale=-UP)
+        window_s = keep.tile([P, T], F32, name="window_s", align_bytes=64)
+        zero = keep.tile([P, 1], F32, name="zero")
+        nc.vector.memset(zero[:], 0.0)
+        nc.scalar.copy(window_s[:, 0:HEAD], zero[:].to_broadcast([P, HEAD]))
+        nc.gpsimd.memset(window_s[:, HEAD:], 0.0)
+        window_v = keep.tile([P, T], F32, name="window_v", align_bytes=64)
+        nc.gpsimd.memset(window_v[:], 0.0)
 
-        warm = keep.tile([P, 1], F32, name="warm")
-        nc.scalar.activation(warm[:], logs[:, PARTS - 1 : PARTS], ACT.Exp)
-
-        gate_row = keep.tile([P, HALF], F32, name="gate_row", align_bytes=64)
-        nc.vector.tensor_copy(gate_row[:], gate_table[:].indirect(entries(0, HALF)))
-
-        picked_rows = keep.tile([P, S], U8, name="picked_rows", tag="rows_then_gate", align_bytes=64)
+        picked_rows = keep.tile([P, S], U8, name="picked_rows", align_bytes=64)
         nc.vector.tensor_copy(picked_rows[:], scale_table[:].indirect(offsets[:]))
-        picked_scales = keep.tile([P, S], U8, name="picked_scales", align_bytes=64)
+
+        gate_row = keep.tile([P, S], F32, name="gate_row", align_bytes=64)
+        for h in range(2):
+            nc.scalar.activation(
+                gate_row[:, h * HALF : (h + 1) * HALF], gate_table[:].indirect(entries(h * HALF, (h + 1) * HALF)), ACT.Copy
+            )
+
+        picked_scales = keep.tile([P, S], U8, name="picked_scales", tag="gate_then_scales", align_bytes=64)
         for q in range(4):
-            nc.sync.dma_start(
+            nc.scalar.dma_start(
                 picked_scales[32 * q : 32 * q + 4 * PASSES, :].bitcast(I32),
                 picked_rows[96 + q : P : 4, :].bitcast(I32),
             )
+
+        per_bank = BANK // P
+        gate_cols = keep.tile([P, S // P], F32, name="gate_cols")
+        for h in range(2):
+            turned = psum.tile([P, per_bank, P], F32, name=f"turned{h}", tag=f"bank{h}")
+            for c in range(per_bank):
+                lo = h * HALF + c * P
+                nc.tensor.transpose(turned[:, c, :], gate_row[:, lo : lo + P], identity[:])
+            nc.scalar.copy(gate_cols[:, h * per_bank : (h + 1) * per_bank], turned[:, :, P - 1])
+
+        picked_words0 = keep.tile([P, S], U32, name="picked_words0", align_bytes=64)
+        nc.vector.tensor_copy(picked_words0[:], word_tables[0][:].bitcast(U32).indirect(offsets[:]))
 
         w_grouped = keep.tile([P, PASSES, N, PACK], BF16, name="w_grouped", tag="grouped_then_words", align_bytes=64)
         nc.scalar.copy(
@@ -103,21 +109,15 @@ def tile_picked_modgate_linnone_p_kernel(tc, x_words, x_scales, gate, w1, offs, 
             w_raw[:].rearrange("p z j (c i) -> p z c j i", i=PACK),
         )
 
-        per_bank = BANK // P
-        log_table = keep.tile([P, T], F32, name="log_table", align_bytes=64)
-
-        def lay_rows(b):
-            rows = psum.tile([P, per_bank, P], F32, name=f"rows{b}", tag=f"bank{b}")
-            for i in range(per_bank):
-                c = b * per_bank + i
-                nc.tensor.transpose(rows[:, i, :], logs[:, PARTS * c : PARTS * c + P], identity[:])
-            nc.scalar.copy(
-                log_table[:].rearrange("p (t c) -> p t c", c=STRIP)[:, :, b * per_bank : (b + 1) * per_bank],
-                rows[:].rearrange("p i t -> p t i"),
-            )
-
-        for b in range(T // BANK):
-            lay_rows(b)
+        spread_gate = []
+        for i, (lo, hi) in enumerate(PIECES):
+            spread = psum.tile([P, hi - lo], F32, name=f"spread{i}", tag=f"bank{2 + i}")
+            for c in range(lo // P, hi // P):
+                nc.tensor.transpose(
+                    spread[:, c * P - lo : (c + 1) * P - lo], gate_cols[:, c : c + 1].to_broadcast([P, P]), identity[:]
+                )
+            spread_gate.append(keep.tile([P, hi - lo], F32, name=f"spread_gate{i}", tag=f"spread_gate{i}", align_bytes=64))
+            nc.scalar.copy(spread_gate[i][:], spread[:])
 
         w_codes = keep.tile([P, PASSES * N], U32, name="w_codes", align_bytes=64)
         w_scales = keep.tile([P, PASSES * N], U8, name="w_scales", align_bytes=64)
@@ -127,78 +127,52 @@ def tile_picked_modgate_linnone_p_kernel(tc, x_words, x_scales, gate, w1, offs, 
             in_=w_grouped[:].rearrange("p z n j -> p (z n j)"),
         )
 
-        picked_words0 = keep.tile([P, S], U32, name="picked_words0", align_bytes=64)
-        nc.vector.tensor_copy(picked_words0[:], word_tables[0][:].bitcast(U32).indirect(offsets[:]))
+        early = PIECES[1][1]
+        words1_early = keep.tile([P, early], U32, name="words1_early", tag="grouped_then_words", align_bytes=64)
 
-        picked_gate = keep.tile([P, S], F32, name="picked_gate", tag="rows_then_gate", align_bytes=64)
-
-        def turn(row, bank):
-            turned = psum.tile([P, per_bank, P], F32, name=f"turned_{bank}", tag=bank)
-            for c in range(per_bank):
-                nc.tensor.transpose(turned[:, c, :], row[:, c * P : (c + 1) * P], identity[:])
-            return turned
-
-        def spread(cols, lo, bank):
-            spread = psum.tile([P, per_bank, P], F32, name=f"spread{lo}", tag=bank)
-            for c in range(per_bank):
-                nc.tensor.transpose(spread[:, c, :], cols[:, c : c + 1].to_broadcast([P, P]), identity[:])
-            nc.scalar.copy(picked_gate[:, lo : lo + HALF], spread[:].rearrange("p c n -> p (c n)"))
-
-        turned = turn(gate_row, "bank0")
-        gate_cols = keep.tile([P, per_bank], F32, name="gate_cols")
-        nc.scalar.copy(gate_cols[:], turned[:, :, P - 1])
-        spread(gate_cols, 0, "bank5")
-
-        picked_parts = keep.tile([P, HALF], F32, name="picked_parts", align_bytes=64)
-        nc.scalar.activation(picked_parts[:], log_table[:].indirect(entries(HALF, S)), ACT.Exp)
-
-        def mx_pass(acc, z, words, lo, hi):
-            nc.tensor.matmul_mx(
-                out=acc[:],
-                lhsT=w_codes[:, z * N : (z + 1) * N].bitcast(FP8X4),
-                lhsT_scale=w_scales[:, z * N : (z + 1) * N],
-                rhs=words.bitcast(FP8X4),
-                rhs_scale=picked_scales[4 * z : P, lo:hi],
-                start=(z == 0),
-                stop=(z == PASSES - 1),
-            )
-
-        y = keep.tile([P, S], F32, name="y", align_bytes=64)
-        picked_words1 = keep.tile([P, S], U32, name="picked_words1", tag="grouped_then_words", align_bytes=64)
-
-        def first_pass(lo, hi, bank):
-            acc = psum.tile([P, hi - lo], F32, name=f"acc{lo}", tag=bank)
-            mx_pass(acc, 0, picked_words0[:, lo:hi], lo, hi)
+        def product(i, words1):
+            lo, hi = PIECES[i]
+            acc = psum.tile([P, hi - lo], F32, name=f"acc{i}", tag=f"bank{5 + i}")
+            cuts = [(a, min(a + 256, hi - lo)) for a in range(0, hi - lo, 256)]
+            for z, words in enumerate((picked_words0[:, lo:hi], words1)):
+                for a, b in cuts:
+                    nc.tensor.matmul_mx(
+                        out=acc[:, a:b],
+                        lhsT=w_codes[:, z * N : (z + 1) * N].bitcast(FP8X4),
+                        lhsT_scale=w_scales[:, z * N : (z + 1) * N],
+                        rhs=words[:, a:b].bitcast(FP8X4),
+                        rhs_scale=picked_scales[4 * z : P, lo + a : lo + b],
+                        start=(z == 0 and a == 0),
+                        stop=(z == PASSES - 1 and b == hi - lo),
+                    )
             return acc
 
-        def gather_words1(lo, hi):
-            nc.vector.tensor_copy(picked_words1[:, lo:hi], word_tables[1][:].bitcast(U32).indirect(entries(lo, hi)))
+        def gather_words1(i, words1):
+            nc.vector.tensor_copy(words1, word_tables[1][:].bitcast(U32).indirect(entries(*PIECES[i])))
 
-        def last_pass(acc, lo, hi):
-            mx_pass(acc, 1, picked_words1[:, lo:hi], lo, hi)
-            nc.scalar.copy(y[:, lo:hi], acc[:])
+        def weigh(i, acc):
+            lo, hi = PIECES[i]
+            weighted = keep.tile([P, hi - lo], F32, name=f"weighted{i}", align_bytes=64)
+            nc.vector.tensor_tensor(weighted[:], acc[:], spread_gate[i][:], ALU.mult)
+            return weighted
 
-        early = [(0, 256), (256, HALF)]
-        accs = [first_pass(lo, hi, f"bank{i + 1}") for i, (lo, hi) in enumerate(early)]
-        for acc, (lo, hi) in zip(accs, early):
-            gather_words1(lo, hi)
-            last_pass(acc, lo, hi)
-        gather_words1(HALF, S)
+        accs = []
+        for i in range(2):
+            lo, hi = PIECES[i]
+            gather_words1(i, words1_early[:, lo:hi])
+            accs.append(product(i, words1_early[:, lo:hi]))
+        weighted = weigh(0, accs[0])
+        nc.scalar.activation(window_s[:].indirect(entries(*PIECES[0])), weighted[:], ACT.Copy)
 
-        turned = turn(picked_parts, "bank5")
-        terms = keep.tile([P, per_bank, PARTS], F32, name="terms")
-        for v, back in enumerate((1 / DOWN, -1 / DOWN, 1 / UP, -1 / UP)):
-            nc.scalar.activation(terms[:, :, v], turned[:, :, v], ACT.Copy, scale=back)
-        late_cols = keep.tile([P, per_bank], F32, name="late_cols")
-        summed = keep.tile([P, per_bank, PARTS], F32, name="summed")
-        for c in range(per_bank):
-            nc.scalar.activation(summed[:, c, :], terms[:, c, :], ACT.Copy, accum_out=late_cols[:, c : c + 1])
-        last_pass(first_pass(HALF, 768, "bank1"), HALF, 768)
-        last_pass(first_pass(768, S, "bank2"), 768, S)
-        spread(late_cols, HALF, "bank7")
+        words1_late = keep.tile([P, S - early], U32, name="words1_late", tag="spread_gate0", align_bytes=64)
+        gather_words1(2, words1_late[:])
+        accs.append(product(2, words1_late[:]))
+        weighted = weigh(1, accs[1])
+        nc.scalar.activation(window_s[:].indirect(entries(*PIECES[1])), weighted[:], ACT.Copy)
+        weighted = weigh(2, accs[2])
+        nc.vector.tensor_copy(window_v[:].indirect(entries(*PIECES[2])), weighted[:])
 
-        for lo, hi in [(0, HALF), (HALF, S)]:
-            nc.vector.tensor_tensor(
-                window[:].indirect(entries(lo, hi)), y[:, lo:hi], picked_gate[:, lo:hi], ALU.mult
-            )
-        nc.sync.dma_start(out, window[:])
+        for lo in range(0, T, STORE):
+            merged = keep.tile([P, STORE], F32, name=f"merged{lo}", align_bytes=64)
+            nc.vector.tensor_tensor(merged[:], window_s[:, lo : lo + STORE], window_v[:, lo : lo + STORE], ALU.add)
+            nc.sync.dma_start(out[:, lo : lo + STORE], merged[:])

@@ -24,7 +24,7 @@ LIST_COLS = 16
 HALF = S // 2
 PIECES = [(0, 256), (256, 640), (640, S)]
 STORE = 512
-HEAD = 512
+HEAD = 768
 
 
 def tile_picked_modgate_linnone_p_kernel(tc, x_words, x_scales, gate, w1, offs, out):
@@ -39,6 +39,9 @@ def tile_picked_modgate_linnone_p_kernel(tc, x_words, x_scales, gate, w1, offs, 
         def entries(lo, hi):
             return offsets[:, lo // LIST_COLS : hi // LIST_COLS]
 
+        zero = keep.tile([P, 1], F32, name="zero")
+        nc.vector.memset(zero[:], 0.0)
+
         scale_table = keep.tile([P, T], U8, name="scale_table", align_bytes=64)
         for z in range(PASSES):
             nc.sync.dma_start(
@@ -50,9 +53,9 @@ def tile_picked_modgate_linnone_p_kernel(tc, x_words, x_scales, gate, w1, offs, 
         identity = keep.tile([P, P], F32, name="identity")
         make_identity(nc, identity[:])
 
-        gate_table = keep.tile([P, T], F32, name="gate_table", tag="gate_then_scales", align_bytes=64)
+        gate_table = keep.tile([P, T], F32, name="gate_table", align_bytes=64)
         nc.sync.dma_start(gate_table[P - 1 : P, :], gate[0:1, :])
-        nc.gpsimd.memset(gate_table[0 : P - 1, :], 0.0)
+        nc.vector.memset(gate_table[0 : P - 1, :], 0.0)
 
         word_tables = [keep.tile([P, T], I32, name=f"word_table{z}", align_bytes=64) for z in range(PASSES)]
         w_raw = keep.tile([P, PASSES, PACK, N], F32, name="w_raw")
@@ -68,12 +71,10 @@ def tile_picked_modgate_linnone_p_kernel(tc, x_words, x_scales, gate, w1, offs, 
         load_words(1)
 
         window_s = keep.tile([P, T], F32, name="window_s", align_bytes=64)
-        zero = keep.tile([P, 1], F32, name="zero")
-        nc.vector.memset(zero[:], 0.0)
         nc.scalar.copy(window_s[:, 0:HEAD], zero[:].to_broadcast([P, HEAD]))
-        nc.gpsimd.memset(window_s[:, HEAD:], 0.0)
+        nc.vector.memset(window_s[:, HEAD:], 0.0)
         window_v = keep.tile([P, T], F32, name="window_v", align_bytes=64)
-        nc.gpsimd.memset(window_v[:], 0.0)
+        nc.vector.memset(window_v[:], 0.0)
 
         picked_rows = keep.tile([P, S], U8, name="picked_rows", align_bytes=64)
         nc.vector.tensor_copy(picked_rows[:], scale_table[:].indirect(offsets[:]))
@@ -84,9 +85,9 @@ def tile_picked_modgate_linnone_p_kernel(tc, x_words, x_scales, gate, w1, offs, 
                 gate_row[:, h * HALF : (h + 1) * HALF], gate_table[:].indirect(entries(h * HALF, (h + 1) * HALF)), ACT.Copy
             )
 
-        picked_scales = keep.tile([P, S], U8, name="picked_scales", tag="gate_then_scales", align_bytes=64)
+        picked_scales = keep.tile([P, S], U8, name="picked_scales", align_bytes=64)
         for q in range(4):
-            nc.scalar.dma_start(
+            nc.sync.dma_start(
                 picked_scales[32 * q : 32 * q + 4 * PASSES, :].bitcast(I32),
                 picked_rows[96 + q : P : 4, :].bitcast(I32),
             )

@@ -58,17 +58,10 @@ def tile_picked_modgate_linnone_p_kernel(tc, x_words, x_scales, gate, w1, offs, 
         nc.vector.memset(gate_table[0 : P - 1, :], 0.0)
 
         word_tables = [keep.tile([P, T], I32, name=f"word_table{z}", align_bytes=64) for z in range(PASSES)]
-        w_raw = keep.tile([P, PASSES, PACK, N], F32, name="w_raw")
-
-        def load_words(z):
+        w_raw = [keep.tile([P, PACK, N], F32, name=f"w_raw{z}") for z in range(PASSES)]
+        for z in range(PASSES):
+            nc.sync.dma_start(w_raw[z][:], w1[z * P * PACK : (z + 1) * P * PACK, :].rearrange("(p j) n -> p j n", j=PACK))
             nc.sync.dma_start(word_tables[z][:], x_words[z].rearrange("p t r -> p (t r)").bitcast(I32))
-
-        load_words(0)
-        nc.sync.dma_start(
-            w_raw[:].rearrange("p z j n -> p z (j n)"),
-            w1.rearrange("(z p j) n -> p z (j n)", z=PASSES, j=PACK),
-        )
-        load_words(1)
 
         window_s = keep.tile([P, T], F32, name="window_s", align_bytes=64)
         nc.scalar.copy(window_s[:, 0:HEAD], zero[:].to_broadcast([P, HEAD]))
@@ -105,10 +98,8 @@ def tile_picked_modgate_linnone_p_kernel(tc, x_words, x_scales, gate, w1, offs, 
         nc.vector.tensor_copy(picked_words0[:], word_tables[0][:].bitcast(U32).indirect(offsets[:]))
 
         w_grouped = keep.tile([P, PASSES, N, PACK], BF16, name="w_grouped", tag="grouped_then_words", align_bytes=64)
-        nc.scalar.copy(
-            w_grouped[:].rearrange("p z (c i) j -> p z c j i", i=PACK),
-            w_raw[:].rearrange("p z j (c i) -> p z c j i", i=PACK),
-        )
+        for z in range(PASSES):
+            nc.scalar.copy(w_grouped[:, z], w_raw[z][:].rearrange("p j n -> p n j"))
 
         spread_gate = []
         for i, (lo, hi) in enumerate(PIECES):

@@ -19,18 +19,19 @@ ACT = mybir.ActivationFunctionType
 P = 128
 PACK = 4
 PASSES = K // (P * PACK)
-BANK = 512
 LIST_COLS = 16
 HALF = S // 2
-PIECES = [(0, 256), (256, 640), (640, S)]
+SUMS = [(0, 256), (256, 640), (640, 896), (896, S)]
+SPREADS = [(0, 256), (256, 640), (640, S)]
 STORE = 512
-HEAD = 768
+HEAD = 256
 
 
 def tile_picked_modgate_linnone_p_kernel(tc, x_words, x_scales, gate, w1, offs, out):
     nc = tc.nc
     with ExitStack() as ctx:
         keep = ctx.enter_context(tc.tile_pool(name="keep", bufs=1))
+        reused = ctx.enter_context(tc.tile_pool(name="reused", bufs=1))
         psum = ctx.enter_context(tc.psum_pool(name="psum", bufs=1))
 
         offsets = keep.tile([P, S // LIST_COLS], U16, name="offsets")
@@ -41,6 +42,10 @@ def tile_picked_modgate_linnone_p_kernel(tc, x_words, x_scales, gate, w1, offs, 
 
         zero = keep.tile([P, 1], F32, name="zero")
         nc.vector.memset(zero[:], 0.0)
+
+        gate_table = keep.tile([P, T], F32, name="gate_table", tag="gate_table", align_bytes=64)
+        nc.sync.dma_start(gate_table[P - 1 : P, :], gate[0:1, :])
+        nc.vector.tensor_copy(gate_table[0 : P - 1, :], zero[0 : P - 1, :].to_broadcast([P - 1, T]))
 
         scale_table = keep.tile([P, T], U8, name="scale_table", align_bytes=64)
         for z in range(PASSES):
@@ -53,116 +58,128 @@ def tile_picked_modgate_linnone_p_kernel(tc, x_words, x_scales, gate, w1, offs, 
         identity = keep.tile([P, P], F32, name="identity")
         make_identity(nc, identity[:])
 
-        gate_table = keep.tile([P, T], F32, name="gate_table", align_bytes=64)
-        nc.sync.dma_start(gate_table[P - 1 : P, :], gate[0:1, :])
-        nc.vector.memset(gate_table[0 : P - 1, :], 0.0)
-
-        word_tables = [keep.tile([P, T], I32, name=f"word_table{z}", align_bytes=64) for z in range(PASSES)]
-        w_raw = [keep.tile([P, PACK, N], F32, name=f"w_raw{z}") for z in range(PASSES)]
+        word_tables = [keep.tile([P, T], I32, name=f"word_table{z}", tag=f"word_table{z}", align_bytes=64) for z in range(PASSES)]
+        w_raw = [reused.tile([P, PACK, N], F32, name=f"w_raw{z}", align_bytes=64, offset=4096 * z) for z in range(PASSES)]
         for z in range(PASSES):
             nc.sync.dma_start(w_raw[z][:], w1[z * P * PACK : (z + 1) * P * PACK, :].rearrange("(p j) n -> p j n", j=PACK))
             nc.sync.dma_start(word_tables[z][:], x_words[z].rearrange("p t r -> p (t r)").bitcast(I32))
 
         window_s = keep.tile([P, T], F32, name="window_s", align_bytes=64)
         nc.scalar.copy(window_s[:, 0:HEAD], zero[:].to_broadcast([P, HEAD]))
-        nc.vector.memset(window_s[:, HEAD:], 0.0)
-        window_v = keep.tile([P, T], F32, name="window_v", align_bytes=64)
-        nc.vector.memset(window_v[:], 0.0)
+        nc.vector.tensor_copy(window_s[:, HEAD:], zero[:].to_broadcast([P, T - HEAD]))
 
         picked_rows = keep.tile([P, S], U8, name="picked_rows", align_bytes=64)
         nc.vector.tensor_copy(picked_rows[:], scale_table[:].indirect(offsets[:]))
 
-        gate_row = keep.tile([P, S], F32, name="gate_row", align_bytes=64)
-        for h in range(2):
-            nc.scalar.activation(
-                gate_row[:, h * HALF : (h + 1) * HALF], gate_table[:].indirect(entries(h * HALF, (h + 1) * HALF)), ACT.Copy
-            )
+        def cast(z, grouped):
+            nc.scalar.copy(grouped[:], w_raw[z][:].rearrange("p j n -> p n j"))
 
-        picked_scales = keep.tile([P, S], U8, name="picked_scales", align_bytes=64)
+        def quantise(z, grouped):
+            codes = keep.tile([P, N], U32, name=f"w_codes{z}", align_bytes=64)
+            scales = keep.tile([P, N], U8, name=f"w_scales{z}", align_bytes=64)
+            nc.vector.quantize_mx(out=codes[:].bitcast(FP8X4), scales=scales[:], in_=grouped[:].rearrange("p n j -> p (n j)"))
+            return codes, scales
+
+        def gather_gate(h, row):
+            nc.scalar.activation(row[:], gate_table[:].indirect(entries(h * HALF, (h + 1) * HALF)), ACT.Copy)
+
+        def turn(h, row, cols):
+            turned = psum.tile([P, HALF // P, P], F32, name=f"turned{h}", tag=f"bank{h}")
+            for c in range(HALF // P):
+                nc.tensor.transpose(turned[:, c, :], row[:, c * P : (c + 1) * P], identity[:])
+            nc.scalar.copy(cols[:], turned[:, :, P - 1])
+
+        row0 = keep.tile([P, HALF], F32, name="gate_row0", align_bytes=64)
+        gather_gate(0, row0)
+        row1 = keep.tile([P, HALF], F32, name="gate_row1", align_bytes=64)
+        gather_gate(1, row1)
+        grouped0 = keep.tile([P, N, PACK], BF16, name="grouped0", tag="grouped0", align_bytes=64)
+        cast(0, grouped0)
+
+        picked_scales = reused.tile([P, S], U8, name="picked_scales", align_bytes=64, offset=0)
         for q in range(4):
-            nc.sync.dma_start(
+            nc.scalar.dma_start(
                 picked_scales[32 * q : 32 * q + 4 * PASSES, :].bitcast(I32),
                 picked_rows[96 + q : P : 4, :].bitcast(I32),
             )
+        window_v = gate_table
+        nc.sync.dma_start(window_v[P - 1 : P, :], window_v[P - 2 : P - 1, :])
+        weights = [quantise(0, grouped0)]
 
-        per_bank = BANK // P
-        gate_cols = keep.tile([P, S // P], F32, name="gate_cols")
-        for h in range(2):
-            turned = psum.tile([P, per_bank, P], F32, name=f"turned{h}", tag=f"bank{h}")
-            for c in range(per_bank):
-                lo = h * HALF + c * P
-                nc.tensor.transpose(turned[:, c, :], gate_row[:, lo : lo + P], identity[:])
-            nc.scalar.copy(gate_cols[:, h * per_bank : (h + 1) * per_bank], turned[:, :, P - 1])
+        words0_first = keep.tile([P, HALF], U32, name="words0_first", tag="grouped0", align_bytes=64)
+        words0_second = keep.tile([P, HALF], U32, name="words0_second", align_bytes=64)
+        nc.vector.tensor_copy(words0_first[:], word_tables[0][:].bitcast(U32).indirect(entries(0, HALF)))
+        nc.vector.tensor_copy(words0_second[:], word_tables[0][:].bitcast(U32).indirect(entries(HALF, S)))
 
-        picked_words0 = keep.tile([P, S], U32, name="picked_words0", align_bytes=64)
-        nc.vector.tensor_copy(picked_words0[:], word_tables[0][:].bitcast(U32).indirect(offsets[:]))
-
-        w_grouped = keep.tile([P, PASSES, N, PACK], BF16, name="w_grouped", tag="grouped_then_words", align_bytes=64)
-        for z in range(PASSES):
-            nc.scalar.copy(w_grouped[:, z], w_raw[z][:].rearrange("p j n -> p n j"))
+        grouped1 = keep.tile([P, N, PACK], BF16, name="grouped1", tag="grouped1", align_bytes=64)
+        cast(1, grouped1)
+        cols = [
+            keep.tile([P, HALF // P], F32, name="gate_cols0"),
+            reused.tile([P, HALF // P], F32, name="gate_cols1", align_bytes=64, offset=1024),
+        ]
+        turn(0, row0, cols[0])
+        turn(1, row1, cols[1])
 
         spread_gate = []
-        for i, (lo, hi) in enumerate(PIECES):
+        for i, (lo, hi) in enumerate(SPREADS):
             spread = psum.tile([P, hi - lo], F32, name=f"spread{i}", tag=f"bank{2 + i}")
             for c in range(lo // P, hi // P):
-                nc.tensor.transpose(
-                    spread[:, c * P - lo : (c + 1) * P - lo], gate_cols[:, c : c + 1].to_broadcast([P, P]), identity[:]
-                )
-            spread_gate.append(keep.tile([P, hi - lo], F32, name=f"spread_gate{i}", tag=f"spread_gate{i}", align_bytes=64))
+                column = cols[c // 4][:, c % 4 : c % 4 + 1]
+                nc.tensor.transpose(spread[:, c * P - lo : (c + 1) * P - lo], column.to_broadcast([P, P]), identity[:])
+            spread_gate.append(reused.tile([P, hi - lo], F32, name=f"spread_gate{i}", align_bytes=64, offset=(1088, 3072, 4608)[i]))
             nc.scalar.copy(spread_gate[i][:], spread[:])
 
-        w_codes = keep.tile([P, PASSES * N], U32, name="w_codes", align_bytes=64)
-        w_scales = keep.tile([P, PASSES * N], U8, name="w_scales", align_bytes=64)
-        nc.vector.quantize_mx(
-            out=w_codes[:].bitcast(FP8X4),
-            scales=w_scales[:],
-            in_=w_grouped[:].rearrange("p z n j -> p (z n j)"),
-        )
+        def multiply(z, acc, base, lo, hi, words, start, stop):
+            codes, scales = weights[z]
+            nc.tensor.matmul_mx(
+                out=acc[:, lo - base : hi - base],
+                lhsT=codes[:].bitcast(FP8X4),
+                lhsT_scale=scales[:],
+                rhs=words.bitcast(FP8X4),
+                rhs_scale=picked_scales[4 * z : P, lo:hi],
+                start=start,
+                stop=stop,
+            )
 
-        early = PIECES[1][1]
-        words1_early = keep.tile([P, early], U32, name="words1_early", tag="grouped_then_words", align_bytes=64)
+        sums = []
+        for i, (lo, hi) in enumerate(SUMS):
+            sums.append(psum.tile([P, hi - lo], F32, name=f"sum{i}", tag=f"bank{(5 + i) % 8}"))
+            cuts = [lo, HALF, hi] if lo < HALF < hi else [lo, hi]
+            for a, b in zip(cuts, cuts[1:]):
+                words = words0_first[:, a:b] if a < HALF else words0_second[:, a - HALF : b - HALF]
+                multiply(0, sums[i], lo, a, b, words, a == lo, False)
 
-        def product(i, words1):
-            lo, hi = PIECES[i]
-            acc = psum.tile([P, hi - lo], F32, name=f"acc{i}", tag=f"bank{5 + i}")
-            cuts = [(a, min(a + 256, hi - lo)) for a in range(0, hi - lo, 256)]
-            for z, words in enumerate((picked_words0[:, lo:hi], words1)):
-                for a, b in cuts:
-                    nc.tensor.matmul_mx(
-                        out=acc[:, a:b],
-                        lhsT=w_codes[:, z * N : (z + 1) * N].bitcast(FP8X4),
-                        lhsT_scale=w_scales[:, z * N : (z + 1) * N],
-                        rhs=words[:, a:b].bitcast(FP8X4),
-                        rhs_scale=picked_scales[4 * z : P, lo + a : lo + b],
-                        start=(z == 0 and a == 0),
-                        stop=(z == PASSES - 1 and b == hi - lo),
-                    )
-            return acc
+        weights.append(quantise(1, grouped1))
 
-        def gather_words1(i, words1):
-            nc.vector.tensor_copy(words1, word_tables[1][:].bitcast(U32).indirect(entries(*PIECES[i])))
+        def second_pass(i, gathers, passes, words):
+            lo, hi = SUMS[i]
+            for a, b in gathers:
+                nc.vector.tensor_copy(words[:, a - lo : b - lo], word_tables[1][:].bitcast(U32).indirect(entries(a, b)))
+                for c, d in passes:
+                    if a <= c and d <= b:
+                        multiply(1, sums[i], lo, c, d, words[:, c - lo : d - lo], False, d == hi)
 
-        def weigh(i, acc):
-            lo, hi = PIECES[i]
-            weighted = keep.tile([P, hi - lo], F32, name=f"weighted{i}", align_bytes=64)
-            nc.vector.tensor_tensor(weighted[:], acc[:], spread_gate[i][:], ALU.mult)
-            return weighted
+        def weigh(i, weighted, gates):
+            nc.vector.tensor_tensor(weighted, sums[i][:], gates, ALU.mult)
 
-        accs = []
-        for i in range(2):
-            lo, hi = PIECES[i]
-            gather_words1(i, words1_early[:, lo:hi])
-            accs.append(product(i, words1_early[:, lo:hi]))
-        weighted = weigh(0, accs[0])
-        nc.scalar.activation(window_s[:].indirect(entries(*PIECES[0])), weighted[:], ACT.Copy)
+        first = keep.tile([P, 256], U32, name="words1_first", tag="grouped1", align_bytes=64)
+        second = keep.tile([P, 384], U32, name="words1_second", align_bytes=64)
+        second_pass(0, [(0, 128), (128, 256)], [(0, 128), (128, 256)], first[:])
+        second_pass(1, [(256, 640)], [(256, 512), (512, 640)], second[:])
+        weighted0 = keep.tile([P, 256], F32, name="weighted0", align_bytes=64)
+        weigh(0, weighted0[:], spread_gate[0][:])
+        nc.scalar.activation(window_s[:].indirect(entries(0, 256)), weighted0[:], ACT.Copy)
 
-        words1_late = keep.tile([P, S - early], U32, name="words1_late", tag="spread_gate0", align_bytes=64)
-        gather_words1(2, words1_late[:])
-        accs.append(product(2, words1_late[:]))
-        weighted = weigh(1, accs[1])
-        nc.scalar.activation(window_s[:].indirect(entries(*PIECES[1])), weighted[:], ACT.Copy)
-        weighted = weigh(2, accs[2])
-        nc.vector.tensor_copy(window_v[:].indirect(entries(*PIECES[2])), weighted[:])
+        late = keep.tile([P, 384], U32, name="words1_late", tag="grouped1", align_bytes=64)
+        second_pass(2, [(640, 896)], [(640, 896)], late[:, 0:256])
+        second_pass(3, [(896, S)], [(896, S)], late[:, 256:384])
+        weighted1 = keep.tile([P, 384], F32, name="weighted1", align_bytes=64)
+        weigh(1, weighted1[:], spread_gate[1][:])
+        nc.scalar.activation(window_s[:].indirect(entries(256, 640)), weighted1[:], ACT.Copy)
+        weighted2 = keep.tile([P, 384], F32, name="weighted2", align_bytes=64)
+        weigh(2, weighted2[:, 0:256], spread_gate[2][:, 0:256])
+        weigh(3, weighted2[:, 256:384], spread_gate[2][:, 256:384])
+        nc.vector.tensor_copy(window_v[:].indirect(entries(640, S)), weighted2[:])
 
         for lo in range(0, T, STORE):
             merged = keep.tile([P, STORE], F32, name=f"merged{lo}", align_bytes=64)

@@ -43,7 +43,7 @@ def tile_picked_modgate_linnone_p_kernel(tc, x_words, x_scales, gate, w1, offs, 
         zero = keep.tile([P, 1], F32, name="zero")
         nc.vector.memset(zero[:], 0.0)
 
-        gate_table = keep.tile([P, T], F32, name="gate_table", tag="gate_table", align_bytes=64)
+        gate_table = keep.tile([P, T], F32, name="gate_table", align_bytes=64)
         nc.sync.dma_start(gate_table[P - 1 : P, :], gate[0:1, :])
         nc.vector.tensor_copy(gate_table[0 : P - 1, :], zero[0 : P - 1, :].to_broadcast([P - 1, T]))
 
@@ -58,8 +58,8 @@ def tile_picked_modgate_linnone_p_kernel(tc, x_words, x_scales, gate, w1, offs, 
         identity = keep.tile([P, P], F32, name="identity")
         make_identity(nc, identity[:])
 
-        word_tables = [keep.tile([P, T], I32, name=f"word_table{z}", tag=f"word_table{z}", align_bytes=64) for z in range(PASSES)]
-        w_raw = [reused.tile([P, PACK, N], F32, name=f"w_raw{z}", align_bytes=64, offset=4096 * z) for z in range(PASSES)]
+        word_tables = [keep.tile([P, T], I32, name=f"word_table{z}", align_bytes=64) for z in range(PASSES)]
+        w_raw = [reused.tile([P, PACK, N], F32, name=f"w_raw{z}", align_bytes=64, offset=(0, 8192)[z]) for z in range(PASSES)]
         for z in range(PASSES):
             nc.sync.dma_start(w_raw[z][:], w1[z * P * PACK : (z + 1) * P * PACK, :].rearrange("(p j) n -> p j n", j=PACK))
             nc.sync.dma_start(word_tables[z][:], x_words[z].rearrange("p t r -> p (t r)").bitcast(I32))
@@ -70,11 +70,16 @@ def tile_picked_modgate_linnone_p_kernel(tc, x_words, x_scales, gate, w1, offs, 
 
         picked_rows = keep.tile([P, S], U8, name="picked_rows", align_bytes=64)
         nc.vector.tensor_copy(picked_rows[:], scale_table[:].indirect(offsets[:]))
+        picked_scales = keep.tile([P, S], U8, name="picked_scales", align_bytes=64)
+        for q in range(4):
+            nc.sync.dma_start(
+                picked_scales[32 * q : 32 * q + 4 * PASSES, :].bitcast(I32),
+                picked_rows[96 + q : P : 4, :].bitcast(I32),
+            )
 
-        def cast(z, grouped):
+        def quantise(z):
+            grouped = keep.tile([P, N, PACK], BF16, name=f"grouped{z}", align_bytes=64)
             nc.scalar.copy(grouped[:], w_raw[z][:].rearrange("p j n -> p n j"))
-
-        def quantise(z, grouped):
             codes = keep.tile([P, N], U32, name=f"w_codes{z}", align_bytes=64)
             scales = keep.tile([P, N], U8, name=f"w_scales{z}", align_bytes=64)
             nc.vector.quantize_mx(out=codes[:].bitcast(FP8X4), scales=scales[:], in_=grouped[:].rearrange("p n j -> p (n j)"))
@@ -83,50 +88,35 @@ def tile_picked_modgate_linnone_p_kernel(tc, x_words, x_scales, gate, w1, offs, 
         def gather_gate(h, row):
             nc.scalar.activation(row[:], gate_table[:].indirect(entries(h * HALF, (h + 1) * HALF)), ACT.Copy)
 
-        def turn(h, row, cols):
+        def turn(h, row):
             turned = psum.tile([P, HALF // P, P], F32, name=f"turned{h}", tag=f"bank{h}")
             for c in range(HALF // P):
                 nc.tensor.transpose(turned[:, c, :], row[:, c * P : (c + 1) * P], identity[:])
+            cols = keep.tile([P, HALF // P], F32, name=f"gate_cols{h}")
             nc.scalar.copy(cols[:], turned[:, :, P - 1])
+            return cols
 
         row0 = keep.tile([P, HALF], F32, name="gate_row0", align_bytes=64)
         gather_gate(0, row0)
-        row1 = keep.tile([P, HALF], F32, name="gate_row1", align_bytes=64)
+        weights = [quantise(0)]
+        row1 = reused.tile([P, HALF], F32, name="gate_row1", align_bytes=64, offset=0)
         gather_gate(1, row1)
-        grouped0 = keep.tile([P, N, PACK], BF16, name="grouped0", tag="grouped0", align_bytes=64)
-        cast(0, grouped0)
 
-        picked_scales = reused.tile([P, S], U8, name="picked_scales", align_bytes=64, offset=0)
-        for q in range(4):
-            nc.scalar.dma_start(
-                picked_scales[32 * q : 32 * q + 4 * PASSES, :].bitcast(I32),
-                picked_rows[96 + q : P : 4, :].bitcast(I32),
-            )
+        words0 = keep.tile([P, S], U32, name="words0", align_bytes=64)
+        nc.vector.tensor_copy(words0[:], word_tables[0][:].bitcast(U32).indirect(offsets[:]))
+        weights.append(quantise(1))
+
         window_v = gate_table
         nc.sync.dma_start(window_v[P - 1 : P, :], window_v[P - 2 : P - 1, :])
-        weights = [quantise(0, grouped0)]
 
-        words0_first = keep.tile([P, HALF], U32, name="words0_first", tag="grouped0", align_bytes=64)
-        words0_second = keep.tile([P, HALF], U32, name="words0_second", align_bytes=64)
-        nc.vector.tensor_copy(words0_first[:], word_tables[0][:].bitcast(U32).indirect(entries(0, HALF)))
-        nc.vector.tensor_copy(words0_second[:], word_tables[0][:].bitcast(U32).indirect(entries(HALF, S)))
-
-        grouped1 = keep.tile([P, N, PACK], BF16, name="grouped1", tag="grouped1", align_bytes=64)
-        cast(1, grouped1)
-        cols = [
-            keep.tile([P, HALF // P], F32, name="gate_cols0"),
-            reused.tile([P, HALF // P], F32, name="gate_cols1", align_bytes=64, offset=1024),
-        ]
-        turn(0, row0, cols[0])
-        turn(1, row1, cols[1])
-
+        cols = [turn(0, row0), turn(1, row1)]
         spread_gate = []
         for i, (lo, hi) in enumerate(SPREADS):
             spread = psum.tile([P, hi - lo], F32, name=f"spread{i}", tag=f"bank{2 + i}")
             for c in range(lo // P, hi // P):
                 column = cols[c // 4][:, c % 4 : c % 4 + 1]
                 nc.tensor.transpose(spread[:, c * P - lo : (c + 1) * P - lo], column.to_broadcast([P, P]), identity[:])
-            spread_gate.append(reused.tile([P, hi - lo], F32, name=f"spread_gate{i}", align_bytes=64, offset=(1088, 3072, 4608)[i]))
+            spread_gate.append(reused.tile([P, hi - lo], F32, name=f"spread_gate{i}", align_bytes=64, offset=(4096, 7168, 8704)[i]))
             nc.scalar.copy(spread_gate[i][:], spread[:])
 
         def multiply(z, acc, base, lo, hi, words, start, stop):
@@ -141,44 +131,35 @@ def tile_picked_modgate_linnone_p_kernel(tc, x_words, x_scales, gate, w1, offs, 
                 stop=stop,
             )
 
-        sums = []
-        for i, (lo, hi) in enumerate(SUMS):
-            sums.append(psum.tile([P, hi - lo], F32, name=f"sum{i}", tag=f"bank{(5 + i) % 8}"))
-            cuts = [lo, HALF, hi] if lo < HALF < hi else [lo, hi]
-            for a, b in zip(cuts, cuts[1:]):
-                words = words0_first[:, a:b] if a < HALF else words0_second[:, a - HALF : b - HALF]
-                multiply(0, sums[i], lo, a, b, words, a == lo, False)
-
-        weights.append(quantise(1, grouped1))
-
-        def second_pass(i, gathers, passes, words):
+        def product(i, gathers, words1):
             lo, hi = SUMS[i]
+            acc = psum.tile([P, hi - lo], F32, name=f"sum{i}", tag=f"bank{(5 + i) % 8}")
+            for a in range(lo, hi, 256):
+                b = min(a + 256, hi)
+                multiply(0, acc, lo, a, b, words0[:, a:b], a == lo, False)
             for a, b in gathers:
-                nc.vector.tensor_copy(words[:, a - lo : b - lo], word_tables[1][:].bitcast(U32).indirect(entries(a, b)))
-                for c, d in passes:
-                    if a <= c and d <= b:
-                        multiply(1, sums[i], lo, c, d, words[:, c - lo : d - lo], False, d == hi)
+                nc.vector.tensor_copy(words1[:, a - lo : b - lo], word_tables[1][:].bitcast(U32).indirect(entries(a, b)))
+                for c in range(a, b, 256):
+                    d = min(c + 256, b)
+                    multiply(1, acc, lo, c, d, words1[:, c - lo : d - lo], False, d == hi)
+            return acc
 
-        def weigh(i, weighted, gates):
-            nc.vector.tensor_tensor(weighted, sums[i][:], gates, ALU.mult)
-
-        first = keep.tile([P, 256], U32, name="words1_first", tag="grouped1", align_bytes=64)
+        first = keep.tile([P, 256], U32, name="words1_first", tag="words1", align_bytes=64)
         second = keep.tile([P, 384], U32, name="words1_second", align_bytes=64)
-        second_pass(0, [(0, 128), (128, 256)], [(0, 128), (128, 256)], first[:])
-        second_pass(1, [(256, 640)], [(256, 512), (512, 640)], second[:])
+        sums = [product(0, [(0, 128), (128, 256)], first[:]), product(1, [(256, 640)], second[:])]
         weighted0 = keep.tile([P, 256], F32, name="weighted0", align_bytes=64)
-        weigh(0, weighted0[:], spread_gate[0][:])
+        nc.vector.tensor_tensor(weighted0[:], sums[0][:], spread_gate[0][:], ALU.mult)
         nc.scalar.activation(window_s[:].indirect(entries(0, 256)), weighted0[:], ACT.Copy)
 
-        late = keep.tile([P, 384], U32, name="words1_late", tag="grouped1", align_bytes=64)
-        second_pass(2, [(640, 896)], [(640, 896)], late[:, 0:256])
-        second_pass(3, [(896, S)], [(896, S)], late[:, 256:384])
+        late = keep.tile([P, 384], U32, name="words1_late", tag="words1", align_bytes=64)
+        sums.append(product(2, [(640, 896)], late[:, 0:256]))
+        sums.append(product(3, [(896, S)], late[:, 256:384]))
         weighted1 = keep.tile([P, 384], F32, name="weighted1", align_bytes=64)
-        weigh(1, weighted1[:], spread_gate[1][:])
+        nc.vector.tensor_tensor(weighted1[:], sums[1][:], spread_gate[1][:], ALU.mult)
         nc.scalar.activation(window_s[:].indirect(entries(256, 640)), weighted1[:], ACT.Copy)
         weighted2 = keep.tile([P, 384], F32, name="weighted2", align_bytes=64)
-        weigh(2, weighted2[:, 0:256], spread_gate[2][:, 0:256])
-        weigh(3, weighted2[:, 256:384], spread_gate[2][:, 256:384])
+        nc.vector.tensor_tensor(weighted2[:, 0:256], sums[2][:], spread_gate[2][:, 0:256], ALU.mult)
+        nc.vector.tensor_tensor(weighted2[:, 256:384], sums[3][:], spread_gate[2][:, 256:384], ALU.mult)
         nc.vector.tensor_copy(window_v[:].indirect(entries(640, S)), weighted2[:])
 
         for lo in range(0, T, STORE):

@@ -44,7 +44,6 @@ def tile_picked_modgate_linnone_p_kernel(tc, x_words, x_scales, gate, w1, offs, 
         nc.vector.memset(zero[:], 0.0)
 
         gate_table = keep.tile([P, T], F32, name="gate_table", align_bytes=64)
-        nc.sync.dma_start(gate_table[P - 1 : P, :], gate[0:1, :])
         nc.vector.tensor_copy(gate_table[0 : P - 1, :], zero[0 : P - 1, :].to_broadcast([P - 1, T]))
 
         scale_table = keep.tile([P, T], U8, name="scale_table", align_bytes=64)
@@ -54,6 +53,7 @@ def tile_picked_modgate_linnone_p_kernel(tc, x_words, x_scales, gate, w1, offs, 
                 x_scales[z].bitcast(I32).rearrange("(q r) c -> r q c", r=4),
             )
         nc.vector.memset(scale_table[0:96, :].bitcast(I32), 0)
+        nc.sync.dma_start(gate_table[P - 1 : P, :], gate[0:1, :])
 
         identity = keep.tile([P, P], F32, name="identity")
         make_identity(nc, identity[:])
@@ -92,7 +92,7 @@ def tile_picked_modgate_linnone_p_kernel(tc, x_words, x_scales, gate, w1, offs, 
             turned = psum.tile([P, HALF // P, P], F32, name=f"turned{h}", tag=f"bank{h}")
             for c in range(HALF // P):
                 nc.tensor.transpose(turned[:, c, :], row[:, c * P : (c + 1) * P], identity[:])
-            cols = keep.tile([P, HALF // P], F32, name=f"gate_cols{h}")
+            cols = reused.tile([P, HALF // P], F32, name=f"gate_cols{h}", align_bytes=64, offset=(4096, 9280)[h])
             nc.scalar.copy(cols[:], turned[:, :, P - 1])
             return cols
 
@@ -116,7 +116,7 @@ def tile_picked_modgate_linnone_p_kernel(tc, x_words, x_scales, gate, w1, offs, 
             for c in range(lo // P, hi // P):
                 column = cols[c // 4][:, c % 4 : c % 4 + 1]
                 nc.tensor.transpose(spread[:, c * P - lo : (c + 1) * P - lo], column.to_broadcast([P, P]), identity[:])
-            spread_gate.append(reused.tile([P, hi - lo], F32, name=f"spread_gate{i}", align_bytes=64, offset=(4096, 7168, 8704)[i]))
+            spread_gate.append(reused.tile([P, hi - lo], F32, name=f"spread_gate{i}", align_bytes=64, offset=(8256, 6720, 9344)[i]))
             nc.scalar.copy(spread_gate[i][:], spread[:])
 
         def multiply(z, acc, base, lo, hi, words, start, stop):

@@ -23,8 +23,8 @@ LIST_COLS = 16
 HALF = S // 2
 SUMS = [(0, 256), (256, 640), (640, 896), (896, S)]
 SPREADS = [(0, 256), (256, 640), (640, S)]
-STORE = 512
-HEAD = 256
+STORES = [256, 256, 384, 384, 384, 384]
+HEAD = 768
 
 
 def tile_picked_modgate_linnone_p_kernel(tc, x_words, x_scales, gate, w1, offs, out):
@@ -162,7 +162,9 @@ def tile_picked_modgate_linnone_p_kernel(tc, x_words, x_scales, gate, w1, offs, 
         nc.vector.tensor_tensor(weighted2[:, 256:384], sums[3][:], spread_gate[2][:, 256:384], ALU.mult)
         nc.vector.tensor_copy(window_v[:].indirect(entries(640, S)), weighted2[:])
 
-        for lo in range(0, T, STORE):
-            merged = keep.tile([P, STORE], F32, name=f"merged{lo}", align_bytes=64)
-            nc.vector.tensor_tensor(merged[:], window_s[:, lo : lo + STORE], window_v[:, lo : lo + STORE], ALU.add)
-            nc.sync.dma_start(out[:, lo : lo + STORE], merged[:])
+        lo = 0
+        for width in STORES:
+            merged = keep.tile([P, width], F32, name=f"merged{lo}", align_bytes=64)
+            nc.vector.tensor_tensor(merged[:], window_s[:, lo : lo + width], window_v[:, lo : lo + width], ALU.add)
+            nc.sync.dma_start(out[:, lo : lo + width], merged[:])
+            lo = lo + width

@@ -163,8 +163,8 @@ def tile_picked_modgate_linnone_p_kernel(tc, x_words, x_scales, gate, w1, offs, 
         nc.vector.tensor_copy(window_v[:].indirect(entries(640, S)), weighted2[:])
 
         lo = 0
-        for width in STORES:
+        for i, width in enumerate(STORES):
             merged = keep.tile([P, width], F32, name=f"merged{lo}", align_bytes=64)
             nc.vector.tensor_tensor(merged[:], window_s[:, lo : lo + width], window_v[:, lo : lo + width], ALU.add)
-            nc.sync.dma_start(out[:, lo : lo + width], merged[:])
+            (nc.sync, nc.scalar)[i % 2].dma_start(out[:, lo : lo + width], merged[:])
             lo = lo + width

@@ -22,9 +22,9 @@ PASSES = K // (P * PACK)
 LIST_COLS = 16
 HALF = S // 2
 SUMS = [(0, 256), (256, 640), (640, 896), (896, S)]
-SPREADS = [(0, 256), (256, 640), (640, S)]
 STORES = [256, 256, 384, 384, 384, 384]
-HEAD = 768
+HEAD = 256
+ROWS = 96
 
 
 def tile_picked_modgate_linnone_p_kernel(tc, x_words, x_scales, gate, w1, offs, out):
@@ -40,100 +40,96 @@ def tile_picked_modgate_linnone_p_kernel(tc, x_words, x_scales, gate, w1, offs, 
         def entries(lo, hi):
             return offsets[:, lo // LIST_COLS : hi // LIST_COLS]
 
-        zero = keep.tile([P, 1], F32, name="zero")
-        nc.vector.memset(zero[:], 0.0)
-
-        gate_table = keep.tile([P, T], F32, name="gate_table", align_bytes=64)
-        nc.vector.tensor_copy(gate_table[0 : P - 1, :], zero[0 : P - 1, :].to_broadcast([P - 1, T]))
-
         scale_table = keep.tile([P, T], U8, name="scale_table", align_bytes=64)
         for z in range(PASSES):
             nc.sync.dma_start(
-                scale_table[96 + 16 * z : 112 + 16 * z, :].bitcast(I32),
+                scale_table[ROWS + 16 * z : ROWS + 16 * (z + 1), :].bitcast(I32),
                 x_scales[z].bitcast(I32).rearrange("(q r) c -> r q c", r=4),
             )
-        nc.vector.memset(scale_table[0:96, :].bitcast(I32), 0)
+        gate_table = keep.tile([P, T], F32, name="gate_table", align_bytes=64)
         nc.sync.dma_start(gate_table[P - 1 : P, :], gate[0:1, :])
+        word_tables = [keep.tile([P, T], I32, name=f"word_table{z}", align_bytes=64) for z in range(PASSES)]
+        w_raw = [reused.tile([P, PACK, N], F32, name=f"w_raw{z}", align_bytes=64, offset=2048 * z) for z in range(PASSES)]
+        nc.sync.dma_start(word_tables[0][:], x_words[0].rearrange("p t r -> p (t r)").bitcast(I32))
+        for z in range(PASSES):
+            nc.sync.dma_start(w_raw[z][:], w1[z * P * PACK : (z + 1) * P * PACK, :].rearrange("(p j) n -> p j n", j=PACK))
+        nc.sync.dma_start(word_tables[1][:], x_words[1].rearrange("p t r -> p (t r)").bitcast(I32))
+
+        zero_s = keep.tile([P, 1], F32, name="zero_s")
+        nc.vector.memset(zero_s[:], 0.0)
+        zero_v = reused.tile([P, 1], F32, name="zero_v", align_bytes=64, offset=16384)
+        nc.vector.memset(zero_v[:], 0.0)
+        nc.vector.memset(scale_table[0:ROWS, :].bitcast(I32), 0)
+        nc.scalar.copy(gate_table[0 : P - 1, 0:HEAD], zero_s[0 : P - 1, :].to_broadcast([P - 1, HEAD]))
+        nc.vector.tensor_copy(gate_table[0 : P - 1, HEAD:], zero_v[0 : P - 1, :].to_broadcast([P - 1, T - HEAD]))
 
         identity = keep.tile([P, P], F32, name="identity")
         make_identity(nc, identity[:])
-
-        word_tables = [keep.tile([P, T], I32, name=f"word_table{z}", align_bytes=64) for z in range(PASSES)]
-        w_raw = [reused.tile([P, PACK, N], F32, name=f"w_raw{z}", align_bytes=64, offset=(0, 8192)[z]) for z in range(PASSES)]
-        for z in range(PASSES):
-            nc.sync.dma_start(w_raw[z][:], w1[z * P * PACK : (z + 1) * P * PACK, :].rearrange("(p j) n -> p j n", j=PACK))
-            nc.sync.dma_start(word_tables[z][:], x_words[z].rearrange("p t r -> p (t r)").bitcast(I32))
-
-        window_s = keep.tile([P, T], F32, name="window_s", align_bytes=64)
-        nc.scalar.copy(window_s[:, 0:HEAD], zero[:].to_broadcast([P, HEAD]))
-        nc.vector.tensor_copy(window_s[:, HEAD:], zero[:].to_broadcast([P, T - HEAD]))
+        window_s = reused.tile([P, T], F32, name="window_s", align_bytes=64, offset=16384)
+        nc.gpsimd.memset(window_s[:], 0.0)
 
         picked_rows = keep.tile([P, S], U8, name="picked_rows", align_bytes=64)
         nc.vector.tensor_copy(picked_rows[:], scale_table[:].indirect(offsets[:]))
-        picked_scales = keep.tile([P, S], U8, name="picked_scales", align_bytes=64)
-        for q in range(4):
-            nc.sync.dma_start(
-                picked_scales[32 * q : 32 * q + 4 * PASSES, :].bitcast(I32),
-                picked_rows[96 + q : P : 4, :].bitcast(I32),
-            )
+        planes = keep.tile([P, S], U8, name="planes", align_bytes=64)
+        for q in (0, 2, 1, 3):
+            nc.sync.dma_start(planes[32 * q : 32 * q + 4 * PASSES, :].bitcast(I32), picked_rows[ROWS + q : P : 4, :].bitcast(I32))
 
-        def quantise(z):
-            grouped = keep.tile([P, N, PACK], BF16, name=f"grouped{z}", align_bytes=64)
-            nc.scalar.copy(grouped[:], w_raw[z][:].rearrange("p j n -> p n j"))
-            codes = keep.tile([P, N], U32, name=f"w_codes{z}", align_bytes=64)
-            scales = keep.tile([P, N], U8, name=f"w_scales{z}", align_bytes=64)
-            nc.vector.quantize_mx(out=codes[:].bitcast(FP8X4), scales=scales[:], in_=grouped[:].rearrange("p n j -> p (n j)"))
-            return codes, scales
+        rows = [
+            keep.tile([P, HALF], F32, name="gate_row0", align_bytes=64),
+            keep.tile([P, HALF], F32, name="gate_row1", align_bytes=64),
+        ]
 
-        def gather_gate(h, row):
-            nc.scalar.activation(row[:], gate_table[:].indirect(entries(h * HALF, (h + 1) * HALF)), ACT.Copy)
+        def gather_gate(h):
+            nc.scalar.activation(rows[h][:], gate_table[:].indirect(entries(h * HALF, (h + 1) * HALF)), ACT.Copy)
 
-        def turn(h, row):
+        def turn(h):
             turned = psum.tile([P, HALF // P, P], F32, name=f"turned{h}", tag=f"bank{h}")
             for c in range(HALF // P):
-                nc.tensor.transpose(turned[:, c, :], row[:, c * P : (c + 1) * P], identity[:])
-            cols = reused.tile([P, HALF // P], F32, name=f"gate_cols{h}", align_bytes=64, offset=(4096, 9280)[h])
+                nc.tensor.transpose(turned[:, c, :], rows[h][:, c * P : (c + 1) * P], identity[:])
+            cols = reused.tile([P, HALF // P], F32, name=f"gate_cols{h}", align_bytes=64, offset=(8192, 0)[h])
             nc.scalar.copy(cols[:], turned[:, :, P - 1])
             return cols
 
-        row0 = keep.tile([P, HALF], F32, name="gate_row0", align_bytes=64)
-        gather_gate(0, row0)
-        weights = [quantise(0)]
-        row1 = reused.tile([P, HALF], F32, name="gate_row1", align_bytes=64, offset=0)
-        gather_gate(1, row1)
+        def spread(h, cols):
+            bank = psum.tile([P, HALF], F32, name=f"spread{h}", tag=f"bank{2 + h}")
+            for c in range(HALF // P):
+                nc.tensor.transpose(bank[:, c * P : (c + 1) * P], cols[:, c : c + 1].to_broadcast([P, P]), identity[:])
+            nc.scalar.copy(scores[:, h * HALF : (h + 1) * HALF], bank[:])
 
+        scores = reused.tile([P, S], F32, name="scores", align_bytes=64, offset=2048)
+        gather_gate(0)
+        gather_gate(1)
+        cols0 = turn(0)
         words0 = keep.tile([P, S], U32, name="words0", align_bytes=64)
         nc.vector.tensor_copy(words0[:], word_tables[0][:].bitcast(U32).indirect(offsets[:]))
-        weights.append(quantise(1))
+
+        grouped = keep.tile([P, PASSES, N, PACK], BF16, name="grouped", align_bytes=64)
+        nc.scalar.copy(grouped[:, 0], w_raw[0][:].rearrange("p j n -> p n j"))
+        cols1 = turn(1)
+        nc.scalar.copy(grouped[:, 1], w_raw[1][:].rearrange("p j n -> p n j"))
+        w_codes = keep.tile([P, PASSES * N], U32, name="w_codes", align_bytes=64)
+        w_scales = keep.tile([P, PASSES * N], U8, name="w_scales", align_bytes=64)
+        nc.vector.quantize_mx(out=w_codes[:].bitcast(FP8X4), scales=w_scales[:], in_=grouped[:].rearrange("p z n j -> p (z n j)"))
+        spread(0, cols0)
+        spread(1, cols1)
 
         window_v = gate_table
         nc.sync.dma_start(window_v[P - 1 : P, :], window_v[P - 2 : P - 1, :])
 
-        cols = [turn(0, row0), turn(1, row1)]
-        spread_gate = []
-        for i, (lo, hi) in enumerate(SPREADS):
-            spread = psum.tile([P, hi - lo], F32, name=f"spread{i}", tag=f"bank{2 + i}")
-            for c in range(lo // P, hi // P):
-                column = cols[c // 4][:, c % 4 : c % 4 + 1]
-                nc.tensor.transpose(spread[:, c * P - lo : (c + 1) * P - lo], column.to_broadcast([P, P]), identity[:])
-            spread_gate.append(reused.tile([P, hi - lo], F32, name=f"spread_gate{i}", align_bytes=64, offset=(8256, 6720, 9344)[i]))
-            nc.scalar.copy(spread_gate[i][:], spread[:])
-
         def multiply(z, acc, base, lo, hi, words, start, stop):
-            codes, scales = weights[z]
             nc.tensor.matmul_mx(
                 out=acc[:, lo - base : hi - base],
-                lhsT=codes[:].bitcast(FP8X4),
-                lhsT_scale=scales[:],
+                lhsT=w_codes[:, z * N : (z + 1) * N].bitcast(FP8X4),
+                lhsT_scale=w_scales[:, z * N : (z + 1) * N],
                 rhs=words.bitcast(FP8X4),
-                rhs_scale=picked_scales[4 * z : P, lo:hi],
+                rhs_scale=planes[4 * z : P, lo:hi],
                 start=start,
                 stop=stop,
             )
 
         def product(i, gathers, words1):
             lo, hi = SUMS[i]
-            acc = psum.tile([P, hi - lo], F32, name=f"sum{i}", tag=f"bank{(5 + i) % 8}")
+            acc = psum.tile([P, hi - lo], F32, name=f"sum{i}", tag=f"bank{4 + i}")
             for a in range(lo, hi, 256):
                 b = min(a + 256, hi)
                 multiply(0, acc, lo, a, b, words0[:, a:b], a == lo, False)
@@ -148,18 +144,18 @@ def tile_picked_modgate_linnone_p_kernel(tc, x_words, x_scales, gate, w1, offs, 
         second = keep.tile([P, 384], U32, name="words1_second", align_bytes=64)
         sums = [product(0, [(0, 128), (128, 256)], first[:]), product(1, [(256, 640)], second[:])]
         weighted0 = keep.tile([P, 256], F32, name="weighted0", align_bytes=64)
-        nc.vector.tensor_tensor(weighted0[:], sums[0][:], spread_gate[0][:], ALU.mult)
+        nc.vector.tensor_tensor(weighted0[:], sums[0][:], scores[:, 0:256], ALU.mult)
         nc.scalar.activation(window_s[:].indirect(entries(0, 256)), weighted0[:], ACT.Copy)
 
         late = keep.tile([P, 384], U32, name="words1_late", tag="words1", align_bytes=64)
         sums.append(product(2, [(640, 896)], late[:, 0:256]))
         sums.append(product(3, [(896, S)], late[:, 256:384]))
         weighted1 = keep.tile([P, 384], F32, name="weighted1", align_bytes=64)
-        nc.vector.tensor_tensor(weighted1[:], sums[1][:], spread_gate[1][:], ALU.mult)
+        nc.vector.tensor_tensor(weighted1[:], sums[1][:], scores[:, 256:640], ALU.mult)
         nc.scalar.activation(window_s[:].indirect(entries(256, 640)), weighted1[:], ACT.Copy)
         weighted2 = keep.tile([P, 384], F32, name="weighted2", align_bytes=64)
-        nc.vector.tensor_tensor(weighted2[:, 0:256], sums[2][:], spread_gate[2][:, 0:256], ALU.mult)
-        nc.vector.tensor_tensor(weighted2[:, 256:384], sums[3][:], spread_gate[2][:, 256:384], ALU.mult)
+        nc.vector.tensor_tensor(weighted2[:, 0:256], sums[2][:], scores[:, 640:896], ALU.mult)
+        nc.vector.tensor_tensor(weighted2[:, 256:384], sums[3][:], scores[:, 896:S], ALU.mult)
         nc.vector.tensor_copy(window_v[:].indirect(entries(640, S)), weighted2[:])
 
         lo = 0

@@ -25,6 +25,7 @@ SUMS = [(0, 256), (256, 640), (640, 896), (896, S)]
 STORES = [256, 256, 384, 384, 384, 384]
 HEAD = 256
 ROWS = 96
+CLEARED = 1024
 
 
 def tile_picked_modgate_linnone_p_kernel(tc, x_words, x_scales, gate, w1, offs, out):
@@ -71,8 +72,12 @@ def tile_picked_modgate_linnone_p_kernel(tc, x_words, x_scales, gate, w1, offs, 
         picked_rows = keep.tile([P, S], U8, name="picked_rows", align_bytes=64)
         nc.vector.tensor_copy(picked_rows[:], scale_table[:].indirect(offsets[:]))
         planes = keep.tile([P, S], U8, name="planes", align_bytes=64)
-        for q in (0, 2, 1, 3):
-            nc.sync.dma_start(planes[32 * q : 32 * q + 4 * PASSES, :].bitcast(I32), picked_rows[ROWS + q : P : 4, :].bitcast(I32))
+        for lo, hi in ((0, 256), (256, S)):
+            for q in (0, 2, 1, 3):
+                queue = nc.gpsimd if (lo, q) == (256, 3) else nc.sync
+                queue.dma_start(
+                    planes[32 * q : 32 * q + 4 * PASSES, lo:hi].bitcast(I32), picked_rows[ROWS + q : P : 4, lo:hi].bitcast(I32)
+                )
 
         rows = [
             keep.tile([P, HALF], F32, name="gate_row0", align_bytes=64),
@@ -96,7 +101,7 @@ def tile_picked_modgate_linnone_p_kernel(tc, x_words, x_scales, gate, w1, offs, 
                 nc.tensor.transpose(bank[:, c * P : (c + 1) * P], cols[:, c : c + 1].to_broadcast([P, P]), identity[:])
             nc.scalar.copy(scores[:, h * HALF : (h + 1) * HALF], bank[:])
 
-        scores = reused.tile([P, S], F32, name="scores", align_bytes=64, offset=2048)
+        scores = reused.tile([P, S], F32, name="scores", align_bytes=64, offset=2112)
         gather_gate(0)
         gather_gate(1)
         cols0 = turn(0)
@@ -114,7 +119,10 @@ def tile_picked_modgate_linnone_p_kernel(tc, x_words, x_scales, gate, w1, offs, 
         spread(1, cols1)
 
         window_v = gate_table
-        nc.sync.dma_start(window_v[P - 1 : P, :], window_v[P - 2 : P - 1, :])
+        nc.gpsimd.memset(window_v[96:P, 0:CLEARED], 0.0)
+        zero_late = reused.tile([P, 1], F32, name="zero_late", align_bytes=64, offset=2048)
+        nc.gpsimd.memset(zero_late[:], 0.0)
+        nc.scalar.copy(window_v[96:P, CLEARED:], zero_late[96:P, :].to_broadcast([P - 96, T - CLEARED]))
 
         def multiply(z, acc, base, lo, hi, words, start, stop):
             nc.tensor.matmul_mx(

from contextlib import ExitStack

import concourse.mybir as mybir
from concourse.masks import make_identity

K, T, S, N = 1024, 2048, 1024, 128
FLOPS = 2 * K * S * N

F32 = mybir.dt.float32
BF16 = mybir.dt.bfloat16
I32 = mybir.dt.int32
U32 = mybir.dt.uint32
U16 = mybir.dt.uint16
U8 = mybir.dt.uint8
FP8X4 = mybir.dt.float8_e4m3fn_x4
ALU = mybir.AluOpType
ACT = mybir.ActivationFunctionType

P = 128
PACK = 4
PASSES = K // (P * PACK)
LIST_COLS = 16
HALF = S // 2
SUMS = [(0, 256), (256, 640), (640, 896), (896, S)]
STORES = [256, 256, 384, 384, 384, 384]
HEAD = 256
ROWS = 96
CLEARED = 1024


def tile_picked_modgate_linnone_p_kernel(tc, x_words, x_scales, gate, w1, offs, out):
    nc = tc.nc
    with ExitStack() as ctx:
        keep = ctx.enter_context(tc.tile_pool(name="keep", bufs=1))
        reused = ctx.enter_context(tc.tile_pool(name="reused", bufs=1))
        psum = ctx.enter_context(tc.psum_pool(name="psum", bufs=1))

        offsets = keep.tile([P, S // LIST_COLS], U16, name="offsets")
        nc.sync.dma_start(offsets[:], offs)

        def entries(lo, hi):
            return offsets[:, lo // LIST_COLS : hi // LIST_COLS]

        scale_table = keep.tile([P, T], U8, name="scale_table", align_bytes=64)
        for z in range(PASSES):
            nc.sync.dma_start(
                scale_table[ROWS + 16 * z : ROWS + 16 * (z + 1), :].bitcast(I32),
                x_scales[z].bitcast(I32).rearrange("(q r) c -> r q c", r=4),
            )
        gate_table = keep.tile([P, T], F32, name="gate_table", align_bytes=64)
        nc.sync.dma_start(gate_table[P - 1 : P, :], gate[0:1, :])
        word_tables = [keep.tile([P, T], I32, name=f"word_table{z}", align_bytes=64) for z in range(PASSES)]
        w_raw = [reused.tile([P, PACK, N], F32, name=f"w_raw{z}", align_bytes=64, offset=2048 * z) for z in range(PASSES)]
        nc.sync.dma_start(word_tables[0][:], x_words[0].rearrange("p t r -> p (t r)").bitcast(I32))
        for z in range(PASSES):
            nc.sync.dma_start(w_raw[z][:], w1[z * P * PACK : (z + 1) * P * PACK, :].rearrange("(p j) n -> p j n", j=PACK))
        nc.sync.dma_start(word_tables[1][:], x_words[1].rearrange("p t r -> p (t r)").bitcast(I32))

        zero_s = keep.tile([P, 1], F32, name="zero_s")
        nc.vector.memset(zero_s[:], 0.0)
        zero_v = reused.tile([P, 1], F32, name="zero_v", align_bytes=64, offset=16384)
        nc.vector.memset(zero_v[:], 0.0)
        nc.vector.memset(scale_table[0:ROWS, :].bitcast(I32), 0)
        nc.scalar.copy(gate_table[0 : P - 1, 0:HEAD], zero_s[0 : P - 1, :].to_broadcast([P - 1, HEAD]))
        nc.vector.tensor_copy(gate_table[0 : P - 1, HEAD:], zero_v[0 : P - 1, :].to_broadcast([P - 1, T - HEAD]))

        identity = keep.tile([P, P], F32, name="identity")
        make_identity(nc, identity[:])
        window_s = reused.tile([P, T], F32, name="window_s", align_bytes=64, offset=16384)
        nc.gpsimd.memset(window_s[:], 0.0)

        picked_rows = keep.tile([P, S], U8, name="picked_rows", align_bytes=64)
        nc.vector.tensor_copy(picked_rows[:], scale_table[:].indirect(offsets[:]))
        planes = keep.tile([P, S], U8, name="planes", align_bytes=64)
        for lo, hi in ((0, 256), (256, S)):
            for q in (0, 2, 1, 3):
                queue = nc.gpsimd if (lo, q) == (256, 3) else nc.sync
                queue.dma_start(
                    planes[32 * q : 32 * q + 4 * PASSES, lo:hi].bitcast(I32), picked_rows[ROWS + q : P : 4, lo:hi].bitcast(I32)
                )

        rows = [
            keep.tile([P, HALF], F32, name="gate_row0", align_bytes=64),
            keep.tile([P, HALF], F32, name="gate_row1", align_bytes=64),
        ]

        def gather_gate(h):
            nc.scalar.activation(rows[h][:], gate_table[:].indirect(entries(h * HALF, (h + 1) * HALF)), ACT.Copy)

        def turn(h):
            turned = psum.tile([P, HALF // P, P], F32, name=f"turned{h}", tag=f"bank{h}")
            for c in range(HALF // P):
                nc.tensor.transpose(turned[:, c, :], rows[h][:, c * P : (c + 1) * P], identity[:])
            cols = reused.tile([P, HALF // P], F32, name=f"gate_cols{h}", align_bytes=64, offset=(8192, 0)[h])
            nc.scalar.copy(cols[:], turned[:, :, P - 1])
            return cols

        def spread(h, cols):
            bank = psum.tile([P, HALF], F32, name=f"spread{h}", tag=f"bank{2 + h}")
            for c in range(HALF // P):
                nc.tensor.transpose(bank[:, c * P : (c + 1) * P], cols[:, c : c + 1].to_broadcast([P, P]), identity[:])
            nc.scalar.copy(scores[:, h * HALF : (h + 1) * HALF], bank[:])

        scores = reused.tile([P, S], F32, name="scores", align_bytes=64, offset=2112)
        gather_gate(0)
        gather_gate(1)
        cols0 = turn(0)
        words0 = keep.tile([P, S], U32, name="words0", align_bytes=64)
        nc.vector.tensor_copy(words0[:], word_tables[0][:].bitcast(U32).indirect(offsets[:]))

        grouped = keep.tile([P, PASSES, N, PACK], BF16, name="grouped", align_bytes=64)
        nc.scalar.copy(grouped[:, 0], w_raw[0][:].rearrange("p j n -> p n j"))
        cols1 = turn(1)
        nc.scalar.copy(grouped[:, 1], w_raw[1][:].rearrange("p j n -> p n j"))
        w_codes = keep.tile([P, PASSES * N], U32, name="w_codes", align_bytes=64)
        w_scales = keep.tile([P, PASSES * N], U8, name="w_scales", align_bytes=64)
        nc.vector.quantize_mx(out=w_codes[:].bitcast(FP8X4), scales=w_scales[:], in_=grouped[:].rearrange("p z n j -> p (z n j)"))
        spread(0, cols0)
        spread(1, cols1)

        window_v = gate_table
        nc.gpsimd.memset(window_v[96:P, 0:CLEARED], 0.0)
        zero_late = reused.tile([P, 1], F32, name="zero_late", align_bytes=64, offset=2048)
        nc.gpsimd.memset(zero_late[:], 0.0)
        nc.scalar.copy(window_v[96:P, CLEARED:], zero_late[96:P, :].to_broadcast([P - 96, T - CLEARED]))

        def multiply(z, acc, base, lo, hi, words, start, stop):
            nc.tensor.matmul_mx(
                out=acc[:, lo - base : hi - base],
                lhsT=w_codes[:, z * N : (z + 1) * N].bitcast(FP8X4),
                lhsT_scale=w_scales[:, z * N : (z + 1) * N],
                rhs=words.bitcast(FP8X4),
                rhs_scale=planes[4 * z : P, lo:hi],
                start=start,
                stop=stop,
            )

        def product(i, gathers, words1):
            lo, hi = SUMS[i]
            acc = psum.tile([P, hi - lo], F32, name=f"sum{i}", tag=f"bank{4 + i}")
            for a in range(lo, hi, 256):
                b = min(a + 256, hi)
                multiply(0, acc, lo, a, b, words0[:, a:b], a == lo, False)
            for a, b in gathers:
                nc.vector.tensor_copy(words1[:, a - lo : b - lo], word_tables[1][:].bitcast(U32).indirect(entries(a, b)))
                for c in range(a, b, 256):
                    d = min(c + 256, b)
                    multiply(1, acc, lo, c, d, words1[:, c - lo : d - lo], False, d == hi)
            return acc

        first = keep.tile([P, 256], U32, name="words1_first", tag="words1", align_bytes=64)
        second = keep.tile([P, 384], U32, name="words1_second", align_bytes=64)
        sums = [product(0, [(0, 128), (128, 256)], first[:]), product(1, [(256, 640)], second[:])]
        weighted0 = keep.tile([P, 256], F32, name="weighted0", align_bytes=64)
        nc.vector.tensor_tensor(weighted0[:], sums[0][:], scores[:, 0:256], ALU.mult)
        nc.scalar.activation(window_s[:].indirect(entries(0, 256)), weighted0[:], ACT.Copy)

        late = keep.tile([P, 384], U32, name="words1_late", tag="words1", align_bytes=64)
        sums.append(product(2, [(640, 896)], late[:, 0:256]))
        sums.append(product(3, [(896, S)], late[:, 256:384]))
        weighted1 = keep.tile([P, 384], F32, name="weighted1", align_bytes=64)
        nc.vector.tensor_tensor(weighted1[:], sums[1][:], scores[:, 256:640], ALU.mult)
        nc.scalar.activation(window_s[:].indirect(entries(256, 640)), weighted1[:], ACT.Copy)
        weighted2 = keep.tile([P, 384], F32, name="weighted2", align_bytes=64)
        nc.vector.tensor_tensor(weighted2[:, 0:256], sums[2][:], scores[:, 640:896], ALU.mult)
        nc.vector.tensor_tensor(weighted2[:, 256:384], sums[3][:], scores[:, 896:S], ALU.mult)
        nc.vector.tensor_copy(window_v[:].indirect(entries(640, S)), weighted2[:])

        lo = 0
        for i, width in enumerate(STORES):
            merged = keep.tile([P, width], F32, name=f"merged{lo}", align_bytes=64)
            nc.vector.tensor_tensor(merged[:], window_s[:, lo : lo + width], window_v[:, lo : lo + width], ALU.add)
            (nc.sync, nc.scalar)[i % 2].dma_start(out[:, lo : lo + width], merged[:])
            lo = lo + width
